import numpy as np
import ml_dtypes


def mxq(x, axis, fmt="e4m3"):
    dtype, down = {"e4m3": (ml_dtypes.float8_e4m3fn, 7), "e5m2": (ml_dtypes.float8_e5m2, 14)}[fmt]
    v = np.moveaxis(np.asarray(x, np.float32).astype(ml_dtypes.bfloat16).astype(np.float64), axis, -1)
    blocks = v.reshape(v.shape[:-1] + (-1, 32))
    amax = np.abs(blocks).max(-1, keepdims=True)
    byte = np.maximum(np.where(amax > 0, np.frexp(amax)[1] - 1 + 127, 0) - down, 1)
    scale = np.exp2(byte - 127.0)
    codes = (blocks / scale).astype(np.float32).astype(dtype).astype(np.float64)
    return np.moveaxis((codes * scale).reshape(v.shape), -1, axis)


WIDE = False


def mx_kscale(k):
    if not WIDE:
        return np.ones(k)
    levels = np.array([10, -10, 5, -5, 0])
    if k % 512:
        return np.exp2(np.random.permutation(np.resize(levels, k // 32))).repeat(32)
    a = np.empty((k // 512, 16))
    for p in range(k // 512):
        a[p, :8] = np.random.permutation(np.resize(levels, 8))
        for g in range(8):
            far = levels[np.abs(levels - a[p, g]) >= 10]
            a[p, g + 8] = far[np.random.randint(len(far))]
    return np.exp2(a.ravel()).repeat(32)


def f64(x):
    return np.asarray(x).astype(np.float64)


def striped(idx):
    return np.tile(idx.reshape(-1, 16).T, (8, 1)).astype(np.uint16)


def unstriped(offs):
    return offs[:16].T.reshape(-1).astype(np.int64)


def striped8(idx):
    return np.concatenate([x.reshape(-1, 16).T for x in idx]).astype(np.uint16)


def runs(offs, k):
    lists = np.stack([offs[16 * r : 16 * r + 16].T.reshape(-1) for r in range(8)]).astype(np.int64)
    return lists[np.arange(k) % 512 // 64]


def pack_weight(w):
    k, n = w.shape
    w = f64(np.asarray(w, np.float32).astype(ml_dtypes.bfloat16)).reshape(k // 32, 32, n)
    amax = np.abs(w).max(1)
    byte = np.clip(np.where(amax > 0, np.frexp(amax)[1] - 1 + 127 - 7, 1), 1, 254)
    scaled = (w * np.exp2(127.0 - byte)[:, None, :]).reshape(k, n).astype(np.float32)
    words = np.ascontiguousarray(scaled.reshape(k // 512, 128, 4, n).transpose(0, 1, 3, 2)).astype(ml_dtypes.float8_e4m3fn).view(np.uint8)
    return words, np.ascontiguousarray(byte.astype(np.uint8).reshape(k // 512, 16, n))


def unpack_weight(words, scales):
    g, p, n, _ = words.shape
    vals = np.ascontiguousarray(words).view(ml_dtypes.float8_e4m3fn).astype(np.float64) * np.repeat(np.exp2(scales.astype(np.float64) - 127.0), 8, axis=1)[..., None]
    return vals.transpose(0, 1, 3, 2).reshape(g * 512, n)

def planes(y):
    n, m = y.shape
    v = y.astype(np.float32).astype(ml_dtypes.bfloat16).astype(np.float64).reshape(n // 32, 32, m)
    top = np.abs(v).max(1)
    byte = np.clip(np.where(top > 0, np.frexp(top)[1] - 1 + 127 - 7, 1), 1, 254)
    codes = (v * np.exp2(127.0 - byte)[:, None, :]).reshape(n, m).astype(np.float32).astype(ml_dtypes.float8_e4m3fn).view(np.uint8)
    words = codes.reshape(n // 512, 128, 4, m).transpose(0, 1, 3, 2)
    return np.ascontiguousarray(words), np.ascontiguousarray(byte.astype(np.uint8).reshape(n // 512, 16, m))


K, T, S, N, U = 512, 2048, 512, 512, 1024


def setup_inputs():
    n = np.random.standard_normal
    s = mx_kscale(K)[:, None]
    packed_xT = pack_weight(n((K, T)) * s)
    return {
        "x_words": packed_xT[0],
        "x_scales": packed_xT[1],
        "w1": (n((K, N)) / np.sqrt(K) / s).astype(np.float32),
        "mem": n((N, U)).astype(np.float32),
        "offs": striped(np.random.permutation(T)[:S]),
        "slot": striped8(np.stack([np.random.permutation(U)[:S] for _ in range(8)])),
        "from_l": striped8(np.random.randint(0, U, (8, S))),
    }


def reference(x_words, x_scales, w1, mem, offs, slot, from_l):
    xq = unpack_weight(x_words, x_scales)[:, unstriped(offs)]
    y = np.tanh(mxq(f64(w1), 0, "e4m3").T @ xq)
    o = y + 0.5 * (f64(mem)[np.arange(N)[:, None], runs(slot, N)] + f64(mem)[np.arange(N)[:, None], runs(from_l, N)])
    out = f64(mem).copy()
    out[np.arange(N)[:, None], runs(slot, N)] = o
    return (out,) + planes(out)

@@ -1,0 +1,157 @@
+from contextlib import ExitStack
+
+import concourse.mybir as mybir
+from concourse.masks import make_identity
+
+K, T, S, N, U = 512, 2048, 512, 512, 1024
+FLOPS = 2 * K * N * S
+
+F32 = mybir.dt.float32
+BF16 = mybir.dt.bfloat16
+I32 = mybir.dt.int32
+U32 = mybir.dt.uint32
+U16 = mybir.dt.uint16
+U8 = mybir.dt.uint8
+FP8X4 = mybir.dt.float8_e4m3fn_x4
+ADD = mybir.AluOpType.add
+COPY = mybir.ActivationFunctionType.Copy
+TANH = mybir.ActivationFunctionType.Tanh
+
+P = 128
+PACK = 4
+PIECES = 4
+PIECE = U // PIECES
+VECTOR_PIECES = 2
+
+
+def tile_picked_slotadd_tanh_po_kernel(
+    tc, x_words, x_scales, w1, mem, offs, slot, from_l, out_0, out_1, out_2
+):
+    nc = tc.nc
+    with ExitStack() as ctx:
+        keep = ctx.enter_context(tc.tile_pool(name="keep", bufs=1))
+        psum = ctx.enter_context(tc.psum_pool(name="psum", bufs=1))
+
+        mem_rows = mem.rearrange("(p t) c -> p t c", t=PACK)
+        out_rows = out_0.rearrange("(p t) c -> p t c", t=PACK)
+        w_rows = w1.rearrange("(p j) c -> p j c", j=PACK)
+
+        slot_list = keep.tile([P, S // 16], U16, name="slot_list")
+        from_list = keep.tile([P, S // 16], U16, name="from_list")
+        token_list = keep.tile([P, S // 16], U16, name="token_list")
+        memory = [keep.tile([P, U], F32, name="memory%d" % t) for t in range(PACK)]
+        w_raw = [keep.tile([P, PACK, N // 2], F32, name="w_raw%d" % h) for h in range(2)]
+        x_table = keep.tile([P, T], I32, name="x_table")
+        x_scale_table = keep.tile([P, T], U8, name="x_scale_table")
+        identity = keep.tile([P, P], F32, name="identity")
+
+        nc.vector.memset(x_scale_table[:].bitcast(I32), 0)
+        make_identity(nc, identity[:])
+
+        nc.sync.dma_start(out=memory[0][:], in_=mem_rows[:, 0, :])
+        nc.sync.dma_start(slot_list[:], slot)
+        nc.sync.dma_start(from_list[:], from_l)
+        nc.sync.dma_start(token_list[:], offs)
+        nc.sync.dma_start(out=w_raw[0][:], in_=w_rows[:, :, 0 : N // 2])
+        nc.sync.dma_start(out=memory[1][:], in_=mem_rows[:, 1, :])
+        nc.sync.dma_start(out=w_raw[1][:], in_=w_rows[:, :, N // 2 : N])
+        nc.sync.dma_start(out=x_table[:], in_=x_words[0].rearrange("p c r -> p (c r)").bitcast(I32))
+        for q in range(4):
+            nc.sync.dma_start(
+                out=x_scale_table[32 * q : 32 * q + 4, :].bitcast(I32),
+                in_=x_scales[0, 4 * q : 4 * q + 4, :].bitcast(I32),
+            )
+        nc.sync.dma_start(out=memory[2][:], in_=mem_rows[:, 2, :])
+        nc.sync.dma_start(out=memory[3][:], in_=mem_rows[:, 3, :])
+
+        halved = {}
+
+        def mean_of_slots(t):
+            at_slot = keep.tile([P, S], F32, name="at_slot%d" % t)
+            at_from = keep.tile([P, S], F32, name="at_from%d" % t)
+            nc.vector.tensor_copy(at_slot[:], memory[t][:].indirect(slot_list[:]))
+            nc.vector.tensor_copy(at_from[:], memory[t][:].indirect(from_list[:]))
+            turned_sum = psum.tile([P, S], F32, name="turned_sum%d" % (t % 2))
+            for b in range(S // P):
+                cols = slice(b * P, (b + 1) * P)
+                nc.tensor.matmul(turned_sum[:, cols], at_slot[:, cols], identity[:], start=True, stop=False, is_transpose=True)
+                nc.tensor.matmul(turned_sum[:, cols], at_from[:, cols], identity[:], start=False, stop=True, is_transpose=True)
+            turned_mean = keep.tile([P, S], F32, name="turned_mean%d" % t)
+            nc.scalar.activation(turned_mean[:], turned_sum[:], COPY, scale=0.5)
+            mean_bank = psum.tile([P, S], F32, name="mean_bank%d" % (t % 2))
+            for b in range(S // P):
+                cols = slice(b * P, (b + 1) * P)
+                nc.tensor.transpose(mean_bank[:, cols], turned_mean[:, cols], identity[:])
+            mean = keep.tile([P, S], F32, name="mean%d" % t)
+            nc.scalar.copy(mean[:], mean_bank[:])
+            halved[t] = mean
+
+        w_grouped = keep.tile([P, N * PACK], BF16, name="w_grouped", align_bytes=64)
+        w_dealt = w_grouped[:].rearrange("p (t m j) -> p m t j", t=PACK, j=PACK)
+        for h in range(2):
+            nc.scalar.copy(
+                w_dealt[:, h * (P // 2) : (h + 1) * (P // 2), :, :],
+                w_raw[h][:].rearrange("p j (m t) -> p m t j", t=PACK),
+            )
+
+        mean_of_slots(0)
+        mean_of_slots(1)
+
+        x_codes = keep.tile([P, S], U32, name="x_codes", align_bytes=64)
+        x_scale = keep.tile([P, S], U8, name="x_scale", align_bytes=64)
+        w_codes = keep.tile([P, N], U32, name="w_codes", align_bytes=64)
+        w_scale = keep.tile([P, N], U8, name="w_scale", align_bytes=64)
+        nc.vector.quantize_mx(out=w_codes[:].bitcast(FP8X4), scales=w_scale[:], in_=w_grouped[:])
+        nc.vector.tensor_copy(x_codes[:], x_table[:].bitcast(U32).indirect(token_list[:]))
+        nc.vector.tensor_copy(x_scale[:], x_scale_table[:].indirect(token_list[:]))
+
+        fresh = []
+        for t in range(PACK):
+            cols = slice(t * P, (t + 1) * P)
+            product = psum.tile([P, S], F32, name="product%d" % t)
+            nc.tensor.matmul_mx(
+                out=product[:],
+                lhsT=w_codes[:, cols].bitcast(FP8X4),
+                lhsT_scale=w_scale[:, cols],
+                rhs=x_codes[:].bitcast(FP8X4),
+                rhs_scale=x_scale[:],
+                start=True,
+                stop=True,
+            )
+            y = keep.tile([P, S], F32, name="y%d" % t)
+            nc.scalar.activation(y[:], product[:], TANH)
+            fresh.append(y)
+
+        mean_of_slots(2)
+        mean_of_slots(3)
+
+        grouped = [keep.tile([P, PIECE, PACK], BF16, name="grouped%d" % i, align_bytes=64) for i in range(PIECES)]
+        for t in range(PACK):
+            nc.vector.tensor_tensor(memory[t][:].indirect(slot_list[:]), fresh[t][:], halved[t][:], ADD)
+            nc.sync.dma_start(out=out_rows[:, t, :], in_=memory[t][:])
+            for i in range(PIECES):
+                source = memory[t][:, i * PIECE : (i + 1) * PIECE]
+                if t == PACK - 1 and i < VECTOR_PIECES:
+                    nc.vector.tensor_copy(grouped[i][:, :, t], source)
+                elif t == PACK - 2 and i < VECTOR_PIECES:
+                    nc.scalar.copy(grouped[i][:, :, t:], source.unsqueeze(2).to_broadcast([P, PIECE, 2]))
+                else:
+                    nc.scalar.copy(grouped[i][:, :, t], source)
+
+        out_scale = keep.tile([P, U], U8, name="out_scale", align_bytes=64)
+        out_words = out_1[0].rearrange("p c r -> p (c r)").bitcast(I32)
+        for i in range(PIECES):
+            cols = slice(i * PIECE, (i + 1) * PIECE)
+            out_codes = keep.tile([P, PIECE], I32, name="out_codes%d" % i, align_bytes=64)
+            nc.vector.quantize_mx(
+                out=out_codes[:].bitcast(FP8X4),
+                scales=out_scale[:, cols],
+                in_=grouped[i][:].rearrange("p c t -> p (c t)"),
+            )
+            nc.sync.dma_start(out=out_words[:, cols], in_=out_codes[:])
+        for q in range(4):
+            queue = nc.scalar if q % 2 == 0 else nc.sync
+            queue.dma_start(
+                out=out_2[0, 4 * q : 4 * q + 4, :].bitcast(I32),
+                in_=out_scale[32 * q : 32 * q + 4, :].bitcast(I32),
+            )

@@ -55,13 +55,13 @@ def tile_picked_slotadd_tanh_po_kernel(
         nc.sync.dma_start(out=w_raw[0][:], in_=w_rows[:, :, 0 : N // 2])
         nc.sync.dma_start(out=memory[1][:], in_=mem_rows[:, 1, :])
         nc.sync.dma_start(out=w_raw[1][:], in_=w_rows[:, :, N // 2 : N])
+        nc.sync.dma_start(out=memory[2][:], in_=mem_rows[:, 2, :])
         nc.sync.dma_start(out=x_table[:], in_=x_words[0].rearrange("p c r -> p (c r)").bitcast(I32))
         for q in range(4):
             nc.sync.dma_start(
                 out=x_scale_table[32 * q : 32 * q + 4, :].bitcast(I32),
                 in_=x_scales[0, 4 * q : 4 * q + 4, :].bitcast(I32),
             )
-        nc.sync.dma_start(out=memory[2][:], in_=mem_rows[:, 2, :])
         nc.sync.dma_start(out=memory[3][:], in_=mem_rows[:, 3, :])
 
         halved = {}
@@ -76,7 +76,7 @@ def tile_picked_slotadd_tanh_po_kernel(
                 cols = slice(b * P, (b + 1) * P)
                 nc.tensor.matmul(turned_sum[:, cols], at_slot[:, cols], identity[:], start=True, stop=False, is_transpose=True)
                 nc.tensor.matmul(turned_sum[:, cols], at_from[:, cols], identity[:], start=False, stop=True, is_transpose=True)
-            turned_mean = keep.tile([P, S], F32, name="turned_mean%d" % t)
+            turned_mean = keep.tile([P, S], F32, name="turned_mean%d" % t, align_bytes=64)
             nc.scalar.activation(turned_mean[:], turned_sum[:], COPY, scale=0.5)
             mean_bank = psum.tile([P, S], F32, name="mean_bank%d" % (t % 2))
             for b in range(S // P):
@@ -96,6 +96,7 @@ def tile_picked_slotadd_tanh_po_kernel(
 
         mean_of_slots(0)
         mean_of_slots(1)
+        mean_of_slots(2)
 
         x_codes = keep.tile([P, S], U32, name="x_codes", align_bytes=64)
         x_scale = keep.tile([P, S], U8, name="x_scale", align_bytes=64)
@@ -122,10 +123,12 @@ def tile_picked_slotadd_tanh_po_kernel(
             nc.scalar.activation(y[:], product[:], TANH)
             fresh.append(y)
 
-        mean_of_slots(2)
         mean_of_slots(3)
 
-        grouped = [keep.tile([P, PIECE, PACK], BF16, name="grouped%d" % i, align_bytes=64) for i in range(PIECES)]
+        rounded = keep.tile([P, U * PACK], BF16, name="rounded", tag="turned_mean3", align_bytes=64)
+        grouped = [
+            rounded[:, i * PIECE * PACK : (i + 1) * PIECE * PACK].rearrange("p (c t) -> p c t", t=PACK) for i in range(PIECES)
+        ]
         for t in range(PACK):
             nc.vector.tensor_tensor(memory[t][:].indirect(slot_list[:]), fresh[t][:], halved[t][:], ADD)
             nc.sync.dma_start(out=out_rows[:, t, :], in_=memory[t][:])
@@ -146,7 +149,7 @@ def tile_picked_slotadd_tanh_po_kernel(
             nc.vector.quantize_mx(
                 out=out_codes[:].bitcast(FP8X4),
                 scales=out_scale[:, cols],
-                in_=grouped[i][:].rearrange("p c t -> p (c t)"),
+                in_=rounded[:, i * PIECE * PACK : (i + 1) * PIECE * PACK],
             )
             nc.sync.dma_start(out=out_words[:, cols], in_=out_codes[:])
         for q in range(4):

@@ -21,7 +21,7 @@ P = 128
 PACK = 4
 PIECES = 4
 PIECE = U // PIECES
-VECTOR_PIECES = 2
+VECTOR_SHARE = 640
 
 
 def tile_picked_slotadd_tanh_po_kernel(
@@ -40,28 +40,28 @@ def tile_picked_slotadd_tanh_po_kernel(
         from_list = keep.tile([P, S // 16], U16, name="from_list")
         token_list = keep.tile([P, S // 16], U16, name="token_list")
         memory = [keep.tile([P, U], F32, name="memory%d" % t) for t in range(PACK)]
-        w_raw = [keep.tile([P, PACK, N // 2], F32, name="w_raw%d" % h) for h in range(2)]
+        w_raw = [keep.tile([P, PACK // 2, N], F32, name="w_raw%d" % h) for h in range(2)]
         x_table = keep.tile([P, T], I32, name="x_table")
         x_scale_table = keep.tile([P, T], U8, name="x_scale_table")
         identity = keep.tile([P, P], F32, name="identity")
 
-        nc.vector.memset(x_scale_table[:].bitcast(I32), 0)
+        nc.gpsimd.memset(x_scale_table[:].bitcast(I32), 0)
         make_identity(nc, identity[:])
 
         nc.sync.dma_start(out=memory[0][:], in_=mem_rows[:, 0, :])
         nc.sync.dma_start(slot_list[:], slot)
         nc.sync.dma_start(from_list[:], from_l)
-        nc.sync.dma_start(token_list[:], offs)
-        nc.sync.dma_start(out=w_raw[0][:], in_=w_rows[:, :, 0 : N // 2])
         nc.sync.dma_start(out=memory[1][:], in_=mem_rows[:, 1, :])
-        nc.sync.dma_start(out=w_raw[1][:], in_=w_rows[:, :, N // 2 : N])
         nc.sync.dma_start(out=memory[2][:], in_=mem_rows[:, 2, :])
-        nc.sync.dma_start(out=x_table[:], in_=x_words[0].rearrange("p c r -> p (c r)").bitcast(I32))
+        nc.sync.dma_start(token_list[:], offs)
         for q in range(4):
             nc.sync.dma_start(
                 out=x_scale_table[32 * q : 32 * q + 4, :].bitcast(I32),
                 in_=x_scales[0, 4 * q : 4 * q + 4, :].bitcast(I32),
             )
+        for h in range(2):
+            nc.sync.dma_start(out=w_raw[h][:], in_=w_rows[:, 2 * h : 2 * h + 2, :])
+        nc.sync.dma_start(out=x_table[:], in_=x_words[0].rearrange("p c r -> p (c r)").bitcast(I32))
         nc.sync.dma_start(out=memory[3][:], in_=mem_rows[:, 3, :])
 
         halved = {}
@@ -90,7 +90,7 @@ def tile_picked_slotadd_tanh_po_kernel(
         w_dealt = w_grouped[:].rearrange("p (t m j) -> p m t j", t=PACK, j=PACK)
         for h in range(2):
             nc.scalar.copy(
-                w_dealt[:, h * (P // 2) : (h + 1) * (P // 2), :, :],
+                w_dealt[:, :, :, 2 * h : 2 * h + 2],
                 w_raw[h][:].rearrange("p j (m t) -> p m t j", t=PACK),
             )
 
@@ -102,9 +102,9 @@ def tile_picked_slotadd_tanh_po_kernel(
         x_scale = keep.tile([P, S], U8, name="x_scale", align_bytes=64)
         w_codes = keep.tile([P, N], U32, name="w_codes", align_bytes=64)
         w_scale = keep.tile([P, N], U8, name="w_scale", align_bytes=64)
+        nc.vector.tensor_copy(x_scale[:], x_scale_table[:].indirect(token_list[:]))
         nc.vector.quantize_mx(out=w_codes[:].bitcast(FP8X4), scales=w_scale[:], in_=w_grouped[:])
         nc.vector.tensor_copy(x_codes[:], x_table[:].bitcast(U32).indirect(token_list[:]))
-        nc.vector.tensor_copy(x_scale[:], x_scale_table[:].indirect(token_list[:]))
 
         fresh = []
         for t in range(PACK):
@@ -126,35 +126,41 @@ def tile_picked_slotadd_tanh_po_kernel(
         mean_of_slots(3)
 
         rounded = keep.tile([P, U * PACK], BF16, name="rounded", tag="turned_mean3", align_bytes=64)
-        grouped = [
-            rounded[:, i * PIECE * PACK : (i + 1) * PIECE * PACK].rearrange("p (c t) -> p c t", t=PACK) for i in range(PIECES)
-        ]
-        for t in range(PACK):
-            nc.vector.tensor_tensor(memory[t][:].indirect(slot_list[:]), fresh[t][:], halved[t][:], ADD)
-            nc.sync.dma_start(out=out_rows[:, t, :], in_=memory[t][:])
-            for i in range(PIECES):
-                source = memory[t][:, i * PIECE : (i + 1) * PIECE]
-                if t == PACK - 1 and i < VECTOR_PIECES:
-                    nc.vector.tensor_copy(grouped[i][:, :, t], source)
-                elif t == PACK - 2 and i < VECTOR_PIECES:
-                    nc.scalar.copy(grouped[i][:, :, t:], source.unsqueeze(2).to_broadcast([P, PIECE, 2]))
-                else:
-                    nc.scalar.copy(grouped[i][:, :, t], source)
-
-        out_scale = keep.tile([P, U], U8, name="out_scale", align_bytes=64)
+        grouped = rounded[:].rearrange("p (c t) -> p c t", t=PACK)
+        out_scale = keep.tile([P, PIECE], U8, name="out_scale", align_bytes=64)
         out_words = out_1[0].rearrange("p c r -> p (c r)").bitcast(I32)
-        for i in range(PIECES):
-            cols = slice(i * PIECE, (i + 1) * PIECE)
+
+        def quantise(i):
             out_codes = keep.tile([P, PIECE], I32, name="out_codes%d" % i, align_bytes=64)
             nc.vector.quantize_mx(
                 out=out_codes[:].bitcast(FP8X4),
-                scales=out_scale[:, cols],
+                scales=out_scale[4 * i : P, :],
                 in_=rounded[:, i * PIECE * PACK : (i + 1) * PIECE * PACK],
             )
-            nc.sync.dma_start(out=out_words[:, cols], in_=out_codes[:])
+            nc.sync.dma_start(out=out_words[:, i * PIECE : (i + 1) * PIECE], in_=out_codes[:])
+
+        for t in range(PACK):
+            nc.vector.tensor_tensor(memory[t][:].indirect(slot_list[:]), fresh[t][:], halved[t][:], ADD)
+            nc.sync.dma_start(out=out_rows[:, t, :], in_=memory[t][:])
+            if t < 2:
+                nc.scalar.copy(grouped[:, :, t], memory[t][:])
+        nc.scalar.copy(
+            grouped[:, :VECTOR_SHARE, 2:], memory[2][:, :VECTOR_SHARE].unsqueeze(2).to_broadcast([P, VECTOR_SHARE, 2])
+        )
+        nc.scalar.copy(grouped[:, VECTOR_SHARE:, 2], memory[2][:, VECTOR_SHARE:])
+
+        nc.scalar.copy(grouped[:, 3 * PIECE :, 3], memory[3][:, 3 * PIECE :])
+        nc.scalar.copy(grouped[:, VECTOR_SHARE : 3 * PIECE, 3], memory[3][:, VECTOR_SHARE : 3 * PIECE])
+        nc.vector.tensor_copy(grouped[:, :PIECE, 3], memory[3][:, :PIECE])
+        nc.vector.tensor_copy(grouped[:, PIECE : 2 * PIECE, 3], memory[3][:, PIECE : 2 * PIECE])
+        quantise(0)
+        nc.vector.tensor_copy(grouped[:, 2 * PIECE : VECTOR_SHARE, 3], memory[3][:, 2 * PIECE : VECTOR_SHARE])
+        quantise(1)
+        quantise(3)
+        quantise(2)
         for q in range(4):
             queue = nc.scalar if q % 2 == 0 else nc.sync
             queue.dma_start(
-                out=out_2[0, 4 * q : 4 * q + 4, :].bitcast(I32),
-                in_=out_scale[32 * q : 32 * q + 4, :].bitcast(I32),
+                out=out_2[0, 4 * q : 4 * q + 4, :].bitcast(I32).rearrange("r (i c) -> i r c", i=PIECES),
+                in_=out_scale[32 * q : 32 * q + 16, :].bitcast(I32),
             )

@@ -21,7 +21,7 @@ P = 128
 PACK = 4
 PIECES = 4
 PIECE = U // PIECES
-VECTOR_SHARE = 640
+VECTOR_SHARE = 512
 
 
 def tile_picked_slotadd_tanh_po_kernel(
@@ -74,14 +74,18 @@ def tile_picked_slotadd_tanh_po_kernel(
             turned_sum = psum.tile([P, S], F32, name="turned_sum%d" % (t % 2))
             for b in range(S // P):
                 cols = slice(b * P, (b + 1) * P)
-                nc.tensor.matmul(turned_sum[:, cols], at_slot[:, cols], identity[:], start=True, stop=False, is_transpose=True)
-                nc.tensor.matmul(turned_sum[:, cols], at_from[:, cols], identity[:], start=False, stop=True, is_transpose=True)
-            turned_mean = keep.tile([P, S], F32, name="turned_mean%d" % t, align_bytes=64)
-            nc.scalar.activation(turned_mean[:], turned_sum[:], COPY, scale=0.5)
+                nc.tensor.matmul(turned_sum[:, cols], at_slot[:, cols], identity[:], start=b == 0, stop=False, is_transpose=True)
+            for b in range(S // P):
+                cols = slice(b * P, (b + 1) * P)
+                nc.tensor.matmul(
+                    turned_sum[:, cols], at_from[:, cols], identity[:], start=False, stop=b == S // P - 1, is_transpose=True
+                )
             mean_bank = psum.tile([P, S], F32, name="mean_bank%d" % (t % 2))
             for b in range(S // P):
                 cols = slice(b * P, (b + 1) * P)
-                nc.tensor.transpose(mean_bank[:, cols], turned_mean[:, cols], identity[:])
+                turned_mean = keep.tile([P, P], F32, name="turned_mean%d_%d" % (t, b), align_bytes=64)
+                nc.scalar.activation(turned_mean[:], turned_sum[:, cols], COPY, scale=0.5)
+                nc.tensor.transpose(mean_bank[:, cols], turned_mean[:], identity[:])
             mean = keep.tile([P, S], F32, name="mean%d" % t)
             nc.scalar.copy(mean[:], mean_bank[:])
             halved[t] = mean
@@ -125,7 +129,7 @@ def tile_picked_slotadd_tanh_po_kernel(
 
         mean_of_slots(3)
 
-        rounded = keep.tile([P, U * PACK], BF16, name="rounded", tag="turned_mean3", align_bytes=64)
+        rounded = keep.tile([P, U * PACK], BF16, name="rounded", tag="turned_mean3_3", align_bytes=64)
         grouped = rounded[:].rearrange("p (c t) -> p c t", t=PACK)
         out_scale = keep.tile([P, PIECE], U8, name="out_scale", align_bytes=64)
         out_words = out_1[0].rearrange("p c r -> p (c r)").bitcast(I32)
@@ -149,15 +153,14 @@ def tile_picked_slotadd_tanh_po_kernel(
         )
         nc.scalar.copy(grouped[:, VECTOR_SHARE:, 2], memory[2][:, VECTOR_SHARE:])
 
-        nc.scalar.copy(grouped[:, 3 * PIECE :, 3], memory[3][:, 3 * PIECE :])
-        nc.scalar.copy(grouped[:, VECTOR_SHARE : 3 * PIECE, 3], memory[3][:, VECTOR_SHARE : 3 * PIECE])
-        nc.vector.tensor_copy(grouped[:, :PIECE, 3], memory[3][:, :PIECE])
-        nc.vector.tensor_copy(grouped[:, PIECE : 2 * PIECE, 3], memory[3][:, PIECE : 2 * PIECE])
-        quantise(0)
-        nc.vector.tensor_copy(grouped[:, 2 * PIECE : VECTOR_SHARE, 3], memory[3][:, 2 * PIECE : VECTOR_SHARE])
-        quantise(1)
-        quantise(3)
-        quantise(2)
+        for i in range(PIECES):
+            cols = slice(i * PIECE, (i + 1) * PIECE)
+            if i * PIECE < VECTOR_SHARE:
+                nc.vector.tensor_copy(grouped[:, cols, 3], memory[3][:, cols])
+            else:
+                nc.scalar.copy(grouped[:, cols, 3], memory[3][:, cols])
+        for i in range(PIECES):
+            quantise(i)
         for q in range(4):
             queue = nc.scalar if q % 2 == 0 else nc.sync
             queue.dma_start(

@@ -21,7 +21,8 @@ P = 128
 PACK = 4
 PIECES = 4
 PIECE = U // PIECES
-VECTOR_SHARE = 512
+VECTOR_SHARE = 576
+STORES = ((0, 512), (512, 768), (768, U))
 
 
 def tile_picked_slotadd_tanh_po_kernel(
@@ -45,33 +46,39 @@ def tile_picked_slotadd_tanh_po_kernel(
         x_scale_table = keep.tile([P, T], U8, name="x_scale_table")
         identity = keep.tile([P, P], F32, name="identity")
 
-        nc.gpsimd.memset(x_scale_table[:].bitcast(I32), 0)
+        x_scale_picked = keep.tile([P, S], U8, name="x_scale_picked")
+        x_scale = keep.tile([P, S], U8, name="x_scale", align_bytes=64)
+        nc.vector.memset(x_scale_table[: P - 16, :].bitcast(I32), 0)
+        nc.vector.memset(x_scale[:].bitcast(I32), 0)
         make_identity(nc, identity[:])
 
+        nc.scalar.dma_start(out=x_scale_table[P - 16 :, :].bitcast(I32), in_=x_scales[0].bitcast(I32))
+        nc.sync.dma_start(token_list[:], offs)
         nc.sync.dma_start(out=memory[0][:], in_=mem_rows[:, 0, :])
         nc.sync.dma_start(slot_list[:], slot)
         nc.sync.dma_start(from_list[:], from_l)
         nc.sync.dma_start(out=memory[1][:], in_=mem_rows[:, 1, :])
-        nc.sync.dma_start(out=memory[2][:], in_=mem_rows[:, 2, :])
-        nc.sync.dma_start(token_list[:], offs)
-        for q in range(4):
-            nc.sync.dma_start(
-                out=x_scale_table[32 * q : 32 * q + 4, :].bitcast(I32),
-                in_=x_scales[0, 4 * q : 4 * q + 4, :].bitcast(I32),
-            )
         for h in range(2):
             nc.sync.dma_start(out=w_raw[h][:], in_=w_rows[:, 2 * h : 2 * h + 2, :])
+        nc.sync.dma_start(out=memory[2][:], in_=mem_rows[:, 2, :])
         nc.sync.dma_start(out=x_table[:], in_=x_words[0].rearrange("p c r -> p (c r)").bitcast(I32))
         nc.sync.dma_start(out=memory[3][:], in_=mem_rows[:, 3, :])
+
+        nc.vector.tensor_copy(x_scale_picked[:], x_scale_table[:].indirect(token_list[:]))
+        for q in range(4):
+            nc.sync.dma_start(
+                out=x_scale[32 * q : 32 * q + 4, :].bitcast(I32),
+                in_=x_scale_picked[P - 16 + 4 * q : P - 12 + 4 * q, :].bitcast(I32),
+            )
 
         halved = {}
 
         def mean_of_slots(t):
-            at_slot = keep.tile([P, S], F32, name="at_slot%d" % t)
-            at_from = keep.tile([P, S], F32, name="at_from%d" % t)
+            at_slot = keep.tile([P, S], F32, name="at_slot%d" % t, tag="w_grouped" if t == 3 else "at_slot%d" % t, align_bytes=64)
+            at_from = keep.tile([P, S], F32, name="at_from%d" % t, tag="x_table" if t == 3 else "at_from%d" % t)
             nc.vector.tensor_copy(at_slot[:], memory[t][:].indirect(slot_list[:]))
             nc.vector.tensor_copy(at_from[:], memory[t][:].indirect(from_list[:]))
-            turned_sum = psum.tile([P, S], F32, name="turned_sum%d" % (t % 2))
+            turned_sum = psum.tile([P, S], F32, name="turned_sum%d" % t, tag="product3" if t == 3 else "turned_sum%d" % (t % 2))
             for b in range(S // P):
                 cols = slice(b * P, (b + 1) * P)
                 nc.tensor.matmul(turned_sum[:, cols], at_slot[:, cols], identity[:], start=b == 0, stop=False, is_transpose=True)
@@ -103,10 +110,8 @@ def tile_picked_slotadd_tanh_po_kernel(
         mean_of_slots(2)
 
         x_codes = keep.tile([P, S], U32, name="x_codes", align_bytes=64)
-        x_scale = keep.tile([P, S], U8, name="x_scale", align_bytes=64)
         w_codes = keep.tile([P, N], U32, name="w_codes", align_bytes=64)
         w_scale = keep.tile([P, N], U8, name="w_scale", align_bytes=64)
-        nc.vector.tensor_copy(x_scale[:], x_scale_table[:].indirect(token_list[:]))
         nc.vector.quantize_mx(out=w_codes[:].bitcast(FP8X4), scales=w_scale[:], in_=w_grouped[:])
         nc.vector.tensor_copy(x_codes[:], x_table[:].bitcast(U32).indirect(token_list[:]))
 
@@ -134,14 +139,21 @@ def tile_picked_slotadd_tanh_po_kernel(
         out_scale = keep.tile([P, PIECE], U8, name="out_scale", align_bytes=64)
         out_words = out_1[0].rearrange("p c r -> p (c r)").bitcast(I32)
 
-        def quantise(i):
-            out_codes = keep.tile([P, PIECE], I32, name="out_codes%d" % i, align_bytes=64)
+        out_codes = [
+            keep.tile([P, last - first], I32, name="out_codes%d" % first, align_bytes=64) for first, last in STORES
+        ]
+
+        def quantise(first, last):
+            n = [first >= a and last <= b for a, b in STORES].index(True)
+            a, b = STORES[n]
+            i = first // PIECE
             nc.vector.quantize_mx(
-                out=out_codes[:].bitcast(FP8X4),
-                scales=out_scale[4 * i : P, :],
-                in_=rounded[:, i * PIECE * PACK : (i + 1) * PIECE * PACK],
+                out=out_codes[n][:, first - a : last - a].bitcast(FP8X4),
+                scales=out_scale[4 * i : P, first - i * PIECE : last - i * PIECE],
+                in_=rounded[:, first * PACK : last * PACK],
             )
-            nc.sync.dma_start(out=out_words[:, i * PIECE : (i + 1) * PIECE], in_=out_codes[:])
+            if last == b:
+                nc.sync.dma_start(out=out_words[:, a:b], in_=out_codes[n][:])
 
         for t in range(PACK):
             nc.vector.tensor_tensor(memory[t][:].indirect(slot_list[:]), fresh[t][:], halved[t][:], ADD)
@@ -153,14 +165,12 @@ def tile_picked_slotadd_tanh_po_kernel(
         )
         nc.scalar.copy(grouped[:, VECTOR_SHARE:, 2], memory[2][:, VECTOR_SHARE:])
 
-        for i in range(PIECES):
-            cols = slice(i * PIECE, (i + 1) * PIECE)
-            if i * PIECE < VECTOR_SHARE:
-                nc.vector.tensor_copy(grouped[:, cols, 3], memory[3][:, cols])
-            else:
-                nc.scalar.copy(grouped[:, cols, 3], memory[3][:, cols])
-        for i in range(PIECES):
-            quantise(i)
+        for first, last in ((0, PIECE), (PIECE, VECTOR_SHARE)):
+            nc.vector.tensor_copy(grouped[:, first:last, 3], memory[3][:, first:last])
+        for first, last in ((VECTOR_SHARE, 768), (768, 896), (896, U)):
+            nc.scalar.copy(grouped[:, first:last, 3], memory[3][:, first:last])
+        for first, last in ((0, 256), (256, 512), (512, 768), (768, 896), (896, U)):
+            quantise(first, last)
         for q in range(4):
             queue = nc.scalar if q % 2 == 0 else nc.sync
             queue.dma_start(

@@ -21,7 +21,7 @@ P = 128
 PACK = 4
 PIECES = 4
 PIECE = U // PIECES
-VECTOR_SHARE = 576
+VECTOR_SHARE = 544
 STORES = ((0, 512), (512, 768), (768, U))
 
 
@@ -52,21 +52,21 @@ def tile_picked_slotadd_tanh_po_kernel(
         nc.vector.memset(x_scale[:].bitcast(I32), 0)
         make_identity(nc, identity[:])
 
-        nc.scalar.dma_start(out=x_scale_table[P - 16 :, :].bitcast(I32), in_=x_scales[0].bitcast(I32))
+        nc.sync.dma_start(out=x_scale_table[P - 16 :, :].bitcast(I32), in_=x_scales[0].bitcast(I32))
         nc.sync.dma_start(token_list[:], offs)
         nc.sync.dma_start(out=memory[0][:], in_=mem_rows[:, 0, :])
         nc.sync.dma_start(slot_list[:], slot)
         nc.sync.dma_start(from_list[:], from_l)
         nc.sync.dma_start(out=memory[1][:], in_=mem_rows[:, 1, :])
-        for h in range(2):
-            nc.sync.dma_start(out=w_raw[h][:], in_=w_rows[:, 2 * h : 2 * h + 2, :])
+        nc.sync.dma_start(out=w_raw[0][:], in_=w_rows[:, 0:2, :])
         nc.sync.dma_start(out=memory[2][:], in_=mem_rows[:, 2, :])
+        nc.sync.dma_start(out=w_raw[1][:], in_=w_rows[:, 2:4, :])
         nc.sync.dma_start(out=x_table[:], in_=x_words[0].rearrange("p c r -> p (c r)").bitcast(I32))
         nc.sync.dma_start(out=memory[3][:], in_=mem_rows[:, 3, :])
 
         nc.vector.tensor_copy(x_scale_picked[:], x_scale_table[:].indirect(token_list[:]))
         for q in range(4):
-            nc.sync.dma_start(
+            nc.gpsimd.dma_start(
                 out=x_scale[32 * q : 32 * q + 4, :].bitcast(I32),
                 in_=x_scale_picked[P - 16 + 4 * q : P - 12 + 4 * q, :].bitcast(I32),
             )
@@ -78,7 +78,7 @@ def tile_picked_slotadd_tanh_po_kernel(
             at_from = keep.tile([P, S], F32, name="at_from%d" % t, tag="x_table" if t == 3 else "at_from%d" % t)
             nc.vector.tensor_copy(at_slot[:], memory[t][:].indirect(slot_list[:]))
             nc.vector.tensor_copy(at_from[:], memory[t][:].indirect(from_list[:]))
-            turned_sum = psum.tile([P, S], F32, name="turned_sum%d" % t, tag="product3" if t == 3 else "turned_sum%d" % (t % 2))
+            turned_sum = psum.tile([P, S], F32, name="turned_sum%d" % t, tag="product0" if t == 3 else "turned_sum%d" % (t % 2))
             for b in range(S // P):
                 cols = slice(b * P, (b + 1) * P)
                 nc.tensor.matmul(turned_sum[:, cols], at_slot[:, cols], identity[:], start=b == 0, stop=False, is_transpose=True)
@@ -88,11 +88,11 @@ def tile_picked_slotadd_tanh_po_kernel(
                     turned_sum[:, cols], at_from[:, cols], identity[:], start=False, stop=b == S // P - 1, is_transpose=True
                 )
             mean_bank = psum.tile([P, S], F32, name="mean_bank%d" % (t % 2))
+            turned_mean = keep.tile([P, S], F32, name="turned_mean%d" % t, align_bytes=64)
+            nc.scalar.activation(turned_mean[:], turned_sum[:], COPY, scale=0.5)
             for b in range(S // P):
                 cols = slice(b * P, (b + 1) * P)
-                turned_mean = keep.tile([P, P], F32, name="turned_mean%d_%d" % (t, b), align_bytes=64)
-                nc.scalar.activation(turned_mean[:], turned_sum[:, cols], COPY, scale=0.5)
-                nc.tensor.transpose(mean_bank[:, cols], turned_mean[:], identity[:])
+                nc.tensor.transpose(mean_bank[:, cols], turned_mean[:, cols], identity[:])
             mean = keep.tile([P, S], F32, name="mean%d" % t)
             nc.scalar.copy(mean[:], mean_bank[:])
             halved[t] = mean
@@ -134,7 +134,7 @@ def tile_picked_slotadd_tanh_po_kernel(
 
         mean_of_slots(3)
 
-        rounded = keep.tile([P, U * PACK], BF16, name="rounded", tag="turned_mean3_3", align_bytes=64)
+        rounded = keep.tile([P, U * PACK], BF16, name="rounded", tag="turned_mean3", align_bytes=64)
         grouped = rounded[:].rearrange("p (c t) -> p c t", t=PACK)
         out_scale = keep.tile([P, PIECE], U8, name="out_scale", align_bytes=64)
         out_words = out_1[0].rearrange("p c r -> p (c r)").bitcast(I32)

@@ -19,10 +19,16 @@ TANH = mybir.ActivationFunctionType.Tanh
 
 P = 128
 PACK = 4
+LAST = PACK - 1
+LIST_ROWS = 16
+SCALE_ROWS = K // 32
+QUADRANTS = 4
 PIECES = 4
 PIECE = U // PIECES
-VECTOR_SHARE = 544
-STORES = ((0, 512), (512, 768), (768, U))
+VECTOR_SHARE = 480
+LAST_HALF = U - PIECE // 2
+QUANTISER_COLUMNS = ((0, PIECE), (PIECE, 2 * PIECE), (2 * PIECE, 3 * PIECE), (3 * PIECE, LAST_HALF), (LAST_HALF, U))
+STORES = ((0, 2 * PIECE), (2 * PIECE, 3 * PIECE), (3 * PIECE, U))
 
 
 def tile_picked_slotadd_tanh_po_kernel(
@@ -37,65 +43,77 @@ def tile_picked_slotadd_tanh_po_kernel(
         out_rows = out_0.rearrange("(p t) c -> p t c", t=PACK)
         w_rows = w1.rearrange("(p j) c -> p j c", j=PACK)
 
-        slot_list = keep.tile([P, S // 16], U16, name="slot_list")
-        from_list = keep.tile([P, S // 16], U16, name="from_list")
-        token_list = keep.tile([P, S // 16], U16, name="token_list")
+        slot_list = keep.tile([P, S // LIST_ROWS], U16, name="slot_list")
+        from_list = keep.tile([P, S // LIST_ROWS], U16, name="from_list")
+        token_list = keep.tile([P, S // LIST_ROWS], U16, name="token_list")
         memory = [keep.tile([P, U], F32, name="memory%d" % t) for t in range(PACK)]
-        w_raw = [keep.tile([P, PACK // 2, N], F32, name="w_raw%d" % h) for h in range(2)]
+        w_raw = [keep.tile([P, PACK // 2, N], F32, name="w_raw%d" % h, align_bytes=64) for h in range(2)]
         x_table = keep.tile([P, T], I32, name="x_table")
         x_scale_table = keep.tile([P, T], U8, name="x_scale_table")
         identity = keep.tile([P, P], F32, name="identity")
 
+        scale_base = P - SCALE_ROWS
         x_scale_picked = keep.tile([P, S], U8, name="x_scale_picked")
         x_scale = keep.tile([P, S], U8, name="x_scale", align_bytes=64)
-        nc.vector.memset(x_scale_table[: P - 16, :].bitcast(I32), 0)
+        nc.vector.memset(x_scale_table[:scale_base, :].bitcast(I32), 0)
         nc.vector.memset(x_scale[:].bitcast(I32), 0)
         make_identity(nc, identity[:])
+        warm = keep.tile([P, 2], F32, name="warm")
+        nc.vector.memset(warm[:, 0:1], 0.0)
+        nc.scalar.activation(warm[:, 1:2], warm[:, 0:1], TANH)
 
-        nc.sync.dma_start(out=x_scale_table[P - 16 :, :].bitcast(I32), in_=x_scales[0].bitcast(I32))
+        nc.sync.dma_start(out=x_scale_table[scale_base:, :].bitcast(I32), in_=x_scales[0].bitcast(I32))
         nc.sync.dma_start(token_list[:], offs)
         nc.sync.dma_start(out=memory[0][:], in_=mem_rows[:, 0, :])
         nc.sync.dma_start(slot_list[:], slot)
         nc.sync.dma_start(from_list[:], from_l)
-        nc.sync.dma_start(out=memory[1][:], in_=mem_rows[:, 1, :])
         nc.sync.dma_start(out=w_raw[0][:], in_=w_rows[:, 0:2, :])
+        nc.sync.dma_start(out=memory[1][:], in_=mem_rows[:, 1, :])
         nc.sync.dma_start(out=memory[2][:], in_=mem_rows[:, 2, :])
         nc.sync.dma_start(out=w_raw[1][:], in_=w_rows[:, 2:4, :])
         nc.sync.dma_start(out=x_table[:], in_=x_words[0].rearrange("p c r -> p (c r)").bitcast(I32))
-        nc.sync.dma_start(out=memory[3][:], in_=mem_rows[:, 3, :])
+        nc.sync.dma_start(out=memory[LAST][:], in_=mem_rows[:, LAST, :])
 
         nc.vector.tensor_copy(x_scale_picked[:], x_scale_table[:].indirect(token_list[:]))
-        for q in range(4):
-            nc.gpsimd.dma_start(
+        for q in range(QUADRANTS):
+            nc.scalar.dma_start(
                 out=x_scale[32 * q : 32 * q + 4, :].bitcast(I32),
-                in_=x_scale_picked[P - 16 + 4 * q : P - 12 + 4 * q, :].bitcast(I32),
+                in_=x_scale_picked[scale_base + 4 * q : scale_base + 4 * q + 4, :].bitcast(I32),
             )
 
-        halved = {}
+        means = {}
 
         def mean_of_slots(t):
-            at_slot = keep.tile([P, S], F32, name="at_slot%d" % t, tag="w_grouped" if t == 3 else "at_slot%d" % t, align_bytes=64)
-            at_from = keep.tile([P, S], F32, name="at_from%d" % t, tag="x_table" if t == 3 else "at_from%d" % t)
+            at_slot = keep.tile(
+                [P, S], F32, name="at_slot%d" % t, tag="w_grouped" if t == LAST else "at_slot%d" % t, align_bytes=64
+            )
+            at_from = keep.tile([P, S], F32, name="at_from%d" % t, tag="x_table" if t == LAST else "at_from%d" % t)
             nc.vector.tensor_copy(at_slot[:], memory[t][:].indirect(slot_list[:]))
             nc.vector.tensor_copy(at_from[:], memory[t][:].indirect(from_list[:]))
-            turned_sum = psum.tile([P, S], F32, name="turned_sum%d" % t, tag="product0" if t == 3 else "turned_sum%d" % (t % 2))
+            turned_sum = psum.tile(
+                [P, S], F32, name="turned_sum%d" % t, tag="product0" if t == LAST else "turned_sum%d" % (t % 2)
+            )
             for b in range(S // P):
                 cols = slice(b * P, (b + 1) * P)
-                nc.tensor.matmul(turned_sum[:, cols], at_slot[:, cols], identity[:], start=b == 0, stop=False, is_transpose=True)
+                nc.tensor.matmul(
+                    turned_sum[:, cols], at_slot[:, cols], identity[:], start=b == 0, stop=False, is_transpose=True
+                )
             for b in range(S // P):
                 cols = slice(b * P, (b + 1) * P)
                 nc.tensor.matmul(
                     turned_sum[:, cols], at_from[:, cols], identity[:], start=False, stop=b == S // P - 1, is_transpose=True
                 )
             mean_bank = psum.tile([P, S], F32, name="mean_bank%d" % (t % 2))
-            turned_mean = keep.tile([P, S], F32, name="turned_mean%d" % t, align_bytes=64)
-            nc.scalar.activation(turned_mean[:], turned_sum[:], COPY, scale=0.5)
-            for b in range(S // P):
-                cols = slice(b * P, (b + 1) * P)
-                nc.tensor.transpose(mean_bank[:, cols], turned_mean[:, cols], identity[:])
+            width = S if t < 2 else P
+            for first in range(0, S, width):
+                name = "turned_mean%d_%d" % (t, first)
+                turned_mean = keep.tile([P, width], F32, name=name, tag="w_raw%d" % t if t < 2 else name, align_bytes=64)
+                nc.scalar.activation(turned_mean[:], turned_sum[:, first : first + width], COPY, scale=0.5)
+                for b in range(0, width, P):
+                    nc.tensor.transpose(mean_bank[:, first + b : first + b + P], turned_mean[:, b : b + P], identity[:])
             mean = keep.tile([P, S], F32, name="mean%d" % t)
             nc.scalar.copy(mean[:], mean_bank[:])
-            halved[t] = mean
+            means[t] = mean
 
         w_grouped = keep.tile([P, N * PACK], BF16, name="w_grouped", align_bytes=64)
         w_dealt = w_grouped[:].rearrange("p (t m j) -> p m t j", t=PACK, j=PACK)
@@ -105,9 +123,8 @@ def tile_picked_slotadd_tanh_po_kernel(
                 w_raw[h][:].rearrange("p j (m t) -> p m t j", t=PACK),
             )
 
-        mean_of_slots(0)
-        mean_of_slots(1)
-        mean_of_slots(2)
+        for t in range(LAST):
+            mean_of_slots(t)
 
         x_codes = keep.tile([P, S], U32, name="x_codes", align_bytes=64)
         w_codes = keep.tile([P, N], U32, name="w_codes", align_bytes=64)
@@ -132,13 +149,14 @@ def tile_picked_slotadd_tanh_po_kernel(
             nc.scalar.activation(y[:], product[:], TANH)
             fresh.append(y)
 
-        mean_of_slots(3)
+        mean_of_slots(LAST)
 
-        rounded = keep.tile([P, U * PACK], BF16, name="rounded", tag="turned_mean3", align_bytes=64)
+        rounded = keep.tile(
+            [P, U * PACK], BF16, name="rounded", tag="turned_mean%d_%d" % (LAST, S - P), align_bytes=64
+        )
         grouped = rounded[:].rearrange("p (c t) -> p c t", t=PACK)
         out_scale = keep.tile([P, PIECE], U8, name="out_scale", align_bytes=64)
         out_words = out_1[0].rearrange("p c r -> p (c r)").bitcast(I32)
-
         out_codes = [
             keep.tile([P, last - first], I32, name="out_codes%d" % first, align_bytes=64) for first, last in STORES
         ]
@@ -156,7 +174,7 @@ def tile_picked_slotadd_tanh_po_kernel(
                 nc.sync.dma_start(out=out_words[:, a:b], in_=out_codes[n][:])
 
         for t in range(PACK):
-            nc.vector.tensor_tensor(memory[t][:].indirect(slot_list[:]), fresh[t][:], halved[t][:], ADD)
+            nc.vector.tensor_tensor(memory[t][:].indirect(slot_list[:]), fresh[t][:], means[t][:], ADD)
             nc.sync.dma_start(out=out_rows[:, t, :], in_=memory[t][:])
             if t < 2:
                 nc.scalar.copy(grouped[:, :, t], memory[t][:])
@@ -166,14 +184,14 @@ def tile_picked_slotadd_tanh_po_kernel(
         nc.scalar.copy(grouped[:, VECTOR_SHARE:, 2], memory[2][:, VECTOR_SHARE:])
 
         for first, last in ((0, PIECE), (PIECE, VECTOR_SHARE)):
-            nc.vector.tensor_copy(grouped[:, first:last, 3], memory[3][:, first:last])
-        for first, last in ((VECTOR_SHARE, 768), (768, 896), (896, U)):
-            nc.scalar.copy(grouped[:, first:last, 3], memory[3][:, first:last])
-        for first, last in ((0, 256), (256, 512), (512, 768), (768, 896), (896, U)):
+            nc.vector.tensor_copy(grouped[:, first:last, LAST], memory[LAST][:, first:last])
+        for first, last in ((VECTOR_SHARE, 3 * PIECE), (3 * PIECE, LAST_HALF), (LAST_HALF, U)):
+            nc.scalar.copy(grouped[:, first:last, LAST], memory[LAST][:, first:last])
+        for first, last in QUANTISER_COLUMNS:
             quantise(first, last)
-        for q in range(4):
+        for q in range(QUADRANTS):
             queue = nc.scalar if q % 2 == 0 else nc.sync
             queue.dma_start(
                 out=out_2[0, 4 * q : 4 * q + 4, :].bitcast(I32).rearrange("r (i c) -> i r c", i=PIECES),
-                in_=out_scale[32 * q : 32 * q + 16, :].bitcast(I32),
+                in_=out_scale[32 * q : 32 * q + 4 * PIECES, :].bitcast(I32),
             )

@@ -14,6 +14,7 @@ U16 = mybir.dt.uint16
 U8 = mybir.dt.uint8
 FP8X4 = mybir.dt.float8_e4m3fn_x4
 ADD = mybir.AluOpType.add
+MULT = mybir.AluOpType.mult
 COPY = mybir.ActivationFunctionType.Copy
 TANH = mybir.ActivationFunctionType.Tanh
 
@@ -48,7 +49,7 @@ def tile_picked_slotadd_tanh_po_kernel(
         token_list = keep.tile([P, S // LIST_ROWS], U16, name="token_list")
         memory = [keep.tile([P, U], F32, name="memory%d" % t) for t in range(PACK)]
         w_raw = [keep.tile([P, PACK // 2, N], F32, name="w_raw%d" % h, align_bytes=64) for h in range(2)]
-        x_table = keep.tile([P, T], I32, name="x_table")
+        x_table = keep.tile([P, T], I32, name="x_table", align_bytes=64)
         x_scale_table = keep.tile([P, T], U8, name="x_scale_table")
         identity = keep.tile([P, P], F32, name="identity")
 
@@ -81,39 +82,39 @@ def tile_picked_slotadd_tanh_po_kernel(
                 in_=x_scale_picked[scale_base + 4 * q : scale_base + 4 * q + 4, :].bitcast(I32),
             )
 
-        means = {}
-
-        def mean_of_slots(t):
-            at_slot = keep.tile(
-                [P, S], F32, name="at_slot%d" % t, tag="w_grouped" if t == LAST else "at_slot%d" % t, align_bytes=64
-            )
-            at_from = keep.tile([P, S], F32, name="at_from%d" % t, tag="x_table" if t == LAST else "at_from%d" % t)
-            nc.vector.tensor_copy(at_slot[:], memory[t][:].indirect(slot_list[:]))
-            nc.vector.tensor_copy(at_from[:], memory[t][:].indirect(from_list[:]))
-            turned_sum = psum.tile(
-                [P, S], F32, name="turned_sum%d" % t, tag="product0" if t == LAST else "turned_sum%d" % (t % 2)
-            )
+        def add_by_transposes(t, first_term, second_term, scale, bank_tag):
+            turned_sum = psum.tile([P, S], F32, name="turned_sum%d" % t, tag=bank_tag)
             for b in range(S // P):
                 cols = slice(b * P, (b + 1) * P)
                 nc.tensor.matmul(
-                    turned_sum[:, cols], at_slot[:, cols], identity[:], start=b == 0, stop=False, is_transpose=True
+                    turned_sum[:, cols], first_term[:, cols], identity[:], start=b == 0, stop=False, is_transpose=True
                 )
             for b in range(S // P):
                 cols = slice(b * P, (b + 1) * P)
                 nc.tensor.matmul(
-                    turned_sum[:, cols], at_from[:, cols], identity[:], start=False, stop=b == S // P - 1, is_transpose=True
+                    turned_sum[:, cols], second_term[:, cols], identity[:], start=False, stop=b == S // P - 1, is_transpose=True
                 )
-            mean_bank = psum.tile([P, S], F32, name="mean_bank%d" % (t % 2))
-            width = S if t < 2 else P
+            back_bank = psum.tile([P, S], F32, name="back_bank%d" % (t % 2))
+            width = P if t == 2 else S
             for first in range(0, S, width):
                 name = "turned_mean%d_%d" % (t, first)
                 turned_mean = keep.tile([P, width], F32, name=name, tag="w_raw%d" % t if t < 2 else name, align_bytes=64)
-                nc.scalar.activation(turned_mean[:], turned_sum[:, first : first + width], COPY, scale=0.5)
+                nc.scalar.activation(turned_mean[:], turned_sum[:, first : first + width], COPY, scale=scale)
                 for b in range(0, width, P):
-                    nc.tensor.transpose(mean_bank[:, first + b : first + b + P], turned_mean[:, b : b + P], identity[:])
-            mean = keep.tile([P, S], F32, name="mean%d" % t)
-            nc.scalar.copy(mean[:], mean_bank[:])
-            means[t] = mean
+                    nc.tensor.transpose(back_bank[:, first + b : first + b + P], turned_mean[:, b : b + P], identity[:])
+            total = keep.tile([P, S], F32, name="total%d" % t)
+            nc.scalar.copy(total[:], back_bank[:])
+            return total
+
+        def gather(name, t, offsets, tag):
+            values = keep.tile([P, S], F32, name=name, tag=tag, align_bytes=64)
+            nc.vector.tensor_copy(values[:], memory[t][:].indirect(offsets[:]))
+            return values
+
+        def gather_half(name, t, offsets, tag):
+            values = keep.tile([P, S], F32, name=name, tag=tag, align_bytes=64)
+            nc.vector.tensor_scalar(values[:], memory[t][:].indirect(offsets[:]), 0.5, 0.0, MULT, ADD)
+            return values
 
         w_grouped = keep.tile([P, N * PACK], BF16, name="w_grouped", align_bytes=64)
         w_dealt = w_grouped[:].rearrange("p (t m j) -> p m t j", t=PACK, j=PACK)
@@ -123,8 +124,11 @@ def tile_picked_slotadd_tanh_po_kernel(
                 w_raw[h][:].rearrange("p j (m t) -> p m t j", t=PACK),
             )
 
+        means = []
         for t in range(LAST):
-            mean_of_slots(t)
+            at_slot = gather("at_slot%d" % t, t, slot_list, "at_slot%d" % t)
+            at_from = gather("at_from%d" % t, t, from_list, "at_from%d" % t)
+            means.append(add_by_transposes(t, at_slot, at_from, 0.5, "turned_sum%d" % (t % 2)))
 
         x_codes = keep.tile([P, S], U32, name="x_codes", align_bytes=64)
         w_codes = keep.tile([P, N], U32, name="w_codes", align_bytes=64)
@@ -132,8 +136,13 @@ def tile_picked_slotadd_tanh_po_kernel(
         nc.vector.quantize_mx(out=w_codes[:].bitcast(FP8X4), scales=w_scale[:], in_=w_grouped[:])
         nc.vector.tensor_copy(x_codes[:], x_table[:].bitcast(U32).indirect(token_list[:]))
 
-        fresh = []
-        for t in range(PACK):
+        half_slot3 = gather_half("half_slot3", LAST, slot_list, "w_grouped")
+        half_from3 = gather_half("half_from3", LAST, from_list, "x_table")
+
+        fresh = {}
+        for t in (0, LAST, 1, 2):
+            if t == 2:
+                partial3 = add_by_transposes(LAST, half_slot3, fresh[LAST], 1.0, "turned_sum1")
             cols = slice(t * P, (t + 1) * P)
             product = psum.tile([P, S], F32, name="product%d" % t)
             nc.tensor.matmul_mx(
@@ -145,17 +154,16 @@ def tile_picked_slotadd_tanh_po_kernel(
                 start=True,
                 stop=True,
             )
-            y = keep.tile([P, S], F32, name="y%d" % t)
+            y = keep.tile([P, S], F32, name="y%d" % t, align_bytes=64)
             nc.scalar.activation(y[:], product[:], TANH)
-            fresh.append(y)
+            fresh[t] = y
 
-        mean_of_slots(LAST)
 
         rounded = keep.tile(
-            [P, U * PACK], BF16, name="rounded", tag="turned_mean%d_%d" % (LAST, S - P), align_bytes=64
+            [P, U * PACK], BF16, name="rounded", tag="turned_mean%d_0" % LAST, align_bytes=64
         )
         grouped = rounded[:].rearrange("p (c t) -> p c t", t=PACK)
-        out_scale = keep.tile([P, PIECE], U8, name="out_scale", align_bytes=64)
+        out_scale = keep.tile([P, U], U8, name="out_scale", align_bytes=64)
         out_words = out_1[0].rearrange("p c r -> p (c r)").bitcast(I32)
         out_codes = [
             keep.tile([P, last - first], I32, name="out_codes%d" % first, align_bytes=64) for first, last in STORES
@@ -164,17 +172,19 @@ def tile_picked_slotadd_tanh_po_kernel(
         def quantise(first, last):
             n = [first >= a and last <= b for a, b in STORES].index(True)
             a, b = STORES[n]
-            i = first // PIECE
             nc.vector.quantize_mx(
                 out=out_codes[n][:, first - a : last - a].bitcast(FP8X4),
-                scales=out_scale[4 * i : P, first - i * PIECE : last - i * PIECE],
+                scales=out_scale[:, first:last],
                 in_=rounded[:, first * PACK : last * PACK],
             )
             if last == b:
                 nc.sync.dma_start(out=out_words[:, a:b], in_=out_codes[n][:])
 
         for t in range(PACK):
-            nc.vector.tensor_tensor(memory[t][:].indirect(slot_list[:]), fresh[t][:], means[t][:], ADD)
+            if t < LAST:
+                nc.vector.tensor_tensor(memory[t][:].indirect(slot_list[:]), fresh[t][:], means[t][:], ADD)
+            else:
+                nc.vector.tensor_tensor(memory[t][:].indirect(slot_list[:]), partial3[:], half_from3[:], ADD)
             nc.sync.dma_start(out=out_rows[:, t, :], in_=memory[t][:])
             if t < 2:
                 nc.scalar.copy(grouped[:, :, t], memory[t][:])
@@ -192,6 +202,6 @@ def tile_picked_slotadd_tanh_po_kernel(
         for q in range(QUADRANTS):
             queue = nc.scalar if q % 2 == 0 else nc.sync
             queue.dma_start(
-                out=out_2[0, 4 * q : 4 * q + 4, :].bitcast(I32).rearrange("r (i c) -> i r c", i=PIECES),
-                in_=out_scale[32 * q : 32 * q + 4 * PIECES, :].bitcast(I32),
+                out=out_2[0, 4 * q : 4 * q + 4, :].bitcast(I32),
+                in_=out_scale[32 * q : 32 * q + 4, :].bitcast(I32),
             )

@@ -1,7 +1,6 @@
 from contextlib import ExitStack
 
 import concourse.mybir as mybir
-from concourse.masks import make_identity
 
 K, T, S, N, U = 512, 2048, 512, 512, 1024
 FLOPS = 2 * K * N * S
@@ -14,7 +13,6 @@ U16 = mybir.dt.uint16
 U8 = mybir.dt.uint8
 FP8X4 = mybir.dt.float8_e4m3fn_x4
 ADD = mybir.AluOpType.add
-MULT = mybir.AluOpType.mult
 COPY = mybir.ActivationFunctionType.Copy
 TANH = mybir.ActivationFunctionType.Tanh
 
@@ -51,14 +49,12 @@ def tile_picked_slotadd_tanh_po_kernel(
         w_raw = [keep.tile([P, PACK // 2, N], F32, name="w_raw%d" % h, align_bytes=64) for h in range(2)]
         x_table = keep.tile([P, T], I32, name="x_table", align_bytes=64)
         x_scale_table = keep.tile([P, T], U8, name="x_scale_table")
-        identity = keep.tile([P, P], F32, name="identity")
 
         scale_base = P - SCALE_ROWS
         x_scale_picked = keep.tile([P, S], U8, name="x_scale_picked")
         x_scale = keep.tile([P, S], U8, name="x_scale", align_bytes=64)
         nc.vector.memset(x_scale_table[:scale_base, :].bitcast(I32), 0)
         nc.vector.memset(x_scale[:].bitcast(I32), 0)
-        make_identity(nc, identity[:])
         warm = keep.tile([P, 2], F32, name="warm")
         nc.vector.memset(warm[:, 0:1], 0.0)
         nc.scalar.activation(warm[:, 1:2], warm[:, 0:1], TANH)
@@ -82,39 +78,19 @@ def tile_picked_slotadd_tanh_po_kernel(
                 in_=x_scale_picked[scale_base + 4 * q : scale_base + 4 * q + 4, :].bitcast(I32),
             )
 
-        def add_by_transposes(t, first_term, second_term, scale, bank_tag):
-            turned_sum = psum.tile([P, S], F32, name="turned_sum%d" % t, tag=bank_tag)
-            for b in range(S // P):
-                cols = slice(b * P, (b + 1) * P)
-                nc.tensor.matmul(
-                    turned_sum[:, cols], first_term[:, cols], identity[:], start=b == 0, stop=False, is_transpose=True
-                )
-            for b in range(S // P):
-                cols = slice(b * P, (b + 1) * P)
-                nc.tensor.matmul(
-                    turned_sum[:, cols], second_term[:, cols], identity[:], start=False, stop=b == S // P - 1, is_transpose=True
-                )
-            back_bank = psum.tile([P, S], F32, name="back_bank%d" % (t % 2))
-            width = P if t == 2 else S
-            for first in range(0, S, width):
-                name = "turned_mean%d_%d" % (t, first)
-                turned_mean = keep.tile([P, width], F32, name=name, tag="w_raw%d" % t if t < 2 else name, align_bytes=64)
-                nc.scalar.activation(turned_mean[:], turned_sum[:, first : first + width], COPY, scale=scale)
-                for b in range(0, width, P):
-                    nc.tensor.transpose(back_bank[:, first + b : first + b + P], turned_mean[:, b : b + P], identity[:])
-            total = keep.tile([P, S], F32, name="total%d" % t)
-            nc.scalar.copy(total[:], back_bank[:])
-            return total
+        halves = [slice(h * S // 2, (h + 1) * S // 2) for h in range(2)]
+        list_halves = [slice(h * S // LIST_ROWS // 2, (h + 1) * S // LIST_ROWS // 2) for h in range(2)]
 
-        def gather(name, t, offsets, tag):
-            values = keep.tile([P, S], F32, name=name, tag=tag, align_bytes=64)
-            nc.vector.tensor_copy(values[:], memory[t][:].indirect(offsets[:]))
-            return values
-
-        def gather_half(name, t, offsets, tag):
-            values = keep.tile([P, S], F32, name=name, tag=tag, align_bytes=64)
-            nc.vector.tensor_scalar(values[:], memory[t][:].indirect(offsets[:]), 0.5, 0.0, MULT, ADD)
-            return values
+        def mean_of_slots(t, mean):
+            at_slot = keep.tile(
+                [P, S], F32, name="at_slot%d" % t, tag="w_grouped" if t == LAST else "at_slot%d" % t, align_bytes=64
+            )
+            both = keep.tile([P, S], F32, name="both%d" % t, tag="x_table" if t == LAST else "both%d" % t, align_bytes=64)
+            for cols, entries in zip(halves, list_halves):
+                nc.vector.tensor_copy(at_slot[:, cols], memory[t][:].indirect(slot_list[:, entries]))
+            for cols, entries in zip(halves, list_halves):
+                nc.vector.tensor_tensor(both[:, cols], memory[t][:].indirect(from_list[:, entries]), at_slot[:, cols], ADD)
+            nc.scalar.activation(mean, both[:], COPY, scale=0.5)
 
         w_grouped = keep.tile([P, N * PACK], BF16, name="w_grouped", align_bytes=64)
         w_dealt = w_grouped[:].rearrange("p (t m j) -> p m t j", t=PACK, j=PACK)
@@ -124,11 +100,10 @@ def tile_picked_slotadd_tanh_po_kernel(
                 w_raw[h][:].rearrange("p j (m t) -> p m t j", t=PACK),
             )
 
-        means = []
+        mean_pairs = [keep.tile([P, 2, S], F32, name="means%d" % h, tag="w_raw%d" % h, align_bytes=64) for h in range(2)]
+        means = [mean_pairs[0][:, 0, :], mean_pairs[1][:, 0, :], mean_pairs[1][:, 1, :], mean_pairs[0][:, 1, :]]
         for t in range(LAST):
-            at_slot = gather("at_slot%d" % t, t, slot_list, "at_slot%d" % t)
-            at_from = gather("at_from%d" % t, t, from_list, "at_from%d" % t)
-            means.append(add_by_transposes(t, at_slot, at_from, 0.5, "turned_sum%d" % (t % 2)))
+            mean_of_slots(t, means[t])
 
         x_codes = keep.tile([P, S], U32, name="x_codes", align_bytes=64)
         w_codes = keep.tile([P, N], U32, name="w_codes", align_bytes=64)
@@ -136,13 +111,8 @@ def tile_picked_slotadd_tanh_po_kernel(
         nc.vector.quantize_mx(out=w_codes[:].bitcast(FP8X4), scales=w_scale[:], in_=w_grouped[:])
         nc.vector.tensor_copy(x_codes[:], x_table[:].bitcast(U32).indirect(token_list[:]))
 
-        half_slot3 = gather_half("half_slot3", LAST, slot_list, "w_grouped")
-        half_from3 = gather_half("half_from3", LAST, from_list, "x_table")
-
         fresh = {}
-        for t in (0, LAST, 1, 2):
-            if t == 2:
-                partial3 = add_by_transposes(LAST, half_slot3, fresh[LAST], 1.0, "turned_sum1")
+        for t in range(PACK):
             cols = slice(t * P, (t + 1) * P)
             product = psum.tile([P, S], F32, name="product%d" % t)
             nc.tensor.matmul_mx(
@@ -159,8 +129,10 @@ def tile_picked_slotadd_tanh_po_kernel(
             fresh[t] = y
 
 
+        mean_of_slots(LAST, means[LAST])
+
         rounded = keep.tile(
-            [P, U * PACK], BF16, name="rounded", tag="turned_mean%d_0" % LAST, align_bytes=64
+            [P, U * PACK], BF16, name="rounded", align_bytes=64
         )
         grouped = rounded[:].rearrange("p (c t) -> p c t", t=PACK)
         out_scale = keep.tile([P, U], U8, name="out_scale", align_bytes=64)
@@ -181,10 +153,7 @@ def tile_picked_slotadd_tanh_po_kernel(
                 nc.sync.dma_start(out=out_words[:, a:b], in_=out_codes[n][:])
 
         for t in range(PACK):
-            if t < LAST:
-                nc.vector.tensor_tensor(memory[t][:].indirect(slot_list[:]), fresh[t][:], means[t][:], ADD)
-            else:
-                nc.vector.tensor_tensor(memory[t][:].indirect(slot_list[:]), partial3[:], half_from3[:], ADD)
+            nc.vector.tensor_tensor(memory[t][:].indirect(slot_list[:]), fresh[t][:], means[t], ADD)
             nc.sync.dma_start(out=out_rows[:, t, :], in_=memory[t][:])
             if t < 2:
                 nc.scalar.copy(grouped[:, :, t], memory[t][:])

@@ -25,6 +25,7 @@ QUADRANTS = 4
 PIECES = 4
 PIECE = U // PIECES
 VECTOR_SHARE = 480
+FILL = 128
 LAST_HALF = U - PIECE // 2
 QUANTISER_COLUMNS = ((0, PIECE), (PIECE, 2 * PIECE), (2 * PIECE, 3 * PIECE), (3 * PIECE, LAST_HALF), (LAST_HALF, U))
 STORES = ((0, 2 * PIECE), (2 * PIECE, 3 * PIECE), (3 * PIECE, U))
@@ -53,19 +54,19 @@ def tile_picked_slotadd_tanh_po_kernel(
         scale_base = P - SCALE_ROWS
         x_scale_picked = keep.tile([P, S], U8, name="x_scale_picked")
         x_scale = keep.tile([P, S], U8, name="x_scale", align_bytes=64)
+        nc.scalar.dma_start(out=x_scale_table[scale_base:, :].bitcast(I32), in_=x_scales[0].bitcast(I32))
         nc.vector.memset(x_scale_table[:scale_base, :].bitcast(I32), 0)
         nc.vector.memset(x_scale[:].bitcast(I32), 0)
         warm = keep.tile([P, 2], F32, name="warm")
         nc.vector.memset(warm[:, 0:1], 0.0)
         nc.scalar.activation(warm[:, 1:2], warm[:, 0:1], TANH)
 
-        nc.sync.dma_start(out=x_scale_table[scale_base:, :].bitcast(I32), in_=x_scales[0].bitcast(I32))
         nc.sync.dma_start(token_list[:], offs)
         nc.sync.dma_start(out=memory[0][:], in_=mem_rows[:, 0, :])
         nc.sync.dma_start(slot_list[:], slot)
         nc.sync.dma_start(from_list[:], from_l)
-        nc.sync.dma_start(out=w_raw[0][:], in_=w_rows[:, 0:2, :])
         nc.sync.dma_start(out=memory[1][:], in_=mem_rows[:, 1, :])
+        nc.sync.dma_start(out=w_raw[0][:], in_=w_rows[:, 0:2, :])
         nc.sync.dma_start(out=memory[2][:], in_=mem_rows[:, 2, :])
         nc.sync.dma_start(out=w_raw[1][:], in_=w_rows[:, 2:4, :])
         nc.sync.dma_start(out=x_table[:], in_=x_words[0].rearrange("p c r -> p (c r)").bitcast(I32))
@@ -132,7 +133,7 @@ def tile_picked_slotadd_tanh_po_kernel(
         mean_of_slots(LAST, means[LAST])
 
         rounded = keep.tile(
-            [P, U * PACK], BF16, name="rounded", align_bytes=64
+            [P, U * PACK], BF16, name="rounded", tag="x_codes", align_bytes=64
         )
         grouped = rounded[:].rearrange("p (c t) -> p c t", t=PACK)
         out_scale = keep.tile([P, U], U8, name="out_scale", align_bytes=64)
@@ -158,10 +159,12 @@ def tile_picked_slotadd_tanh_po_kernel(
             if t < 2:
                 nc.scalar.copy(grouped[:, :, t], memory[t][:])
         nc.scalar.copy(
-            grouped[:, :VECTOR_SHARE, 2:], memory[2][:, :VECTOR_SHARE].unsqueeze(2).to_broadcast([P, VECTOR_SHARE, 2])
+            grouped[:, FILL:VECTOR_SHARE, 2:],
+            memory[2][:, FILL:VECTOR_SHARE].unsqueeze(2).to_broadcast([P, VECTOR_SHARE - FILL, 2]),
         )
         nc.scalar.copy(grouped[:, VECTOR_SHARE:, 2], memory[2][:, VECTOR_SHARE:])
 
+        nc.vector.tensor_copy(grouped[:, :FILL, 2], memory[2][:, :FILL])
         for first, last in ((0, PIECE), (PIECE, VECTOR_SHARE)):
             nc.vector.tensor_copy(grouped[:, first:last, LAST], memory[LAST][:, first:last])
         for first, last in ((VECTOR_SHARE, 3 * PIECE), (3 * PIECE, LAST_HALF), (LAST_HALF, U)):

@@ -28,7 +28,7 @@ VECTOR_SHARE = 480
 FILL = 128
 LAST_HALF = U - PIECE // 2
 QUANTISER_COLUMNS = ((0, PIECE), (PIECE, 2 * PIECE), (2 * PIECE, 3 * PIECE), (3 * PIECE, LAST_HALF), (LAST_HALF, U))
-STORES = ((0, 2 * PIECE), (2 * PIECE, 3 * PIECE), (3 * PIECE, U))
+STORES = tuple((first, first + PIECE) for first in range(0, U, PIECE))
 
 
 def tile_picked_slotadd_tanh_po_kernel(

@@ -57,9 +57,6 @@ def tile_picked_slotadd_tanh_po_kernel(
         nc.scalar.dma_start(out=x_scale_table[scale_base:, :].bitcast(I32), in_=x_scales[0].bitcast(I32))
         nc.vector.memset(x_scale_table[:scale_base, :].bitcast(I32), 0)
         nc.vector.memset(x_scale[:].bitcast(I32), 0)
-        warm = keep.tile([P, 2], F32, name="warm")
-        nc.vector.memset(warm[:, 0:1], 0.0)
-        nc.scalar.activation(warm[:, 1:2], warm[:, 0:1], TANH)
 
         nc.sync.dma_start(token_list[:], offs)
         nc.sync.dma_start(out=memory[0][:], in_=mem_rows[:, 0, :])

@@ -13,6 +13,7 @@ U16 = mybir.dt.uint16
 U8 = mybir.dt.uint8
 FP8X4 = mybir.dt.float8_e4m3fn_x4
 ADD = mybir.AluOpType.add
+MULT = mybir.AluOpType.mult
 COPY = mybir.ActivationFunctionType.Copy
 TANH = mybir.ActivationFunctionType.Tanh
 
@@ -22,13 +23,10 @@ LAST = PACK - 1
 LIST_ROWS = 16
 SCALE_ROWS = K // 32
 QUADRANTS = 4
-PIECES = 4
-PIECE = U // PIECES
-VECTOR_SHARE = 480
-FILL = 128
-LAST_HALF = U - PIECE // 2
-QUANTISER_COLUMNS = ((0, PIECE), (PIECE, 2 * PIECE), (2 * PIECE, 3 * PIECE), (3 * PIECE, LAST_HALF), (LAST_HALF, U))
-STORES = tuple((first, first + PIECE) for first in range(0, U, PIECE))
+PIECES = ((0, 128), (128, 384), (384, 640), (640, 768), (768, 896), (896, U))
+STORES = ((0, 384), (384, 640), (640, 896), (896, U))
+SCALAR_WEAVES = 2
+W_VECTOR = 80
 
 
 def tile_picked_slotadd_tanh_po_kernel(
@@ -46,15 +44,18 @@ def tile_picked_slotadd_tanh_po_kernel(
         slot_list = keep.tile([P, S // LIST_ROWS], U16, name="slot_list")
         from_list = keep.tile([P, S // LIST_ROWS], U16, name="from_list")
         token_list = keep.tile([P, S // LIST_ROWS], U16, name="token_list")
-        memory = [keep.tile([P, U], F32, name="memory%d" % t) for t in range(PACK)]
+        memory = [keep.tile([P, U], F32, name="memory0", align_bytes=64)]
         w_raw = [keep.tile([P, PACK // 2, N], F32, name="w_raw%d" % h, align_bytes=64) for h in range(2)]
         x_table = keep.tile([P, T], I32, name="x_table", align_bytes=64)
-        x_scale_table = keep.tile([P, T], U8, name="x_scale_table")
+        x_scale_table = keep.tile([P, T], U8, name="x_scale_table", align_bytes=64)
 
         scale_base = P - SCALE_ROWS
-        x_scale_picked = keep.tile([P, S], U8, name="x_scale_picked")
+        x_scale_picked = keep.tile([P, S], U8, name="x_scale_picked", align_bytes=64)
         x_scale = keep.tile([P, S], U8, name="x_scale", align_bytes=64)
         nc.scalar.dma_start(out=x_scale_table[scale_base:, :].bitcast(I32), in_=x_scales[0].bitcast(I32))
+        warm = keep.tile([P, 2], F32, name="warm")
+        nc.vector.memset(warm[:, 0:1], 0.0)
+        nc.scalar.activation(warm[:, 1:2], warm[:, 0:1], TANH)
         nc.vector.memset(x_scale_table[:scale_base, :].bitcast(I32), 0)
         nc.vector.memset(x_scale[:].bitcast(I32), 0)
 
@@ -62,112 +63,122 @@ def tile_picked_slotadd_tanh_po_kernel(
         nc.sync.dma_start(out=memory[0][:], in_=mem_rows[:, 0, :])
         nc.sync.dma_start(slot_list[:], slot)
         nc.sync.dma_start(from_list[:], from_l)
-        nc.sync.dma_start(out=memory[1][:], in_=mem_rows[:, 1, :])
         nc.sync.dma_start(out=w_raw[0][:], in_=w_rows[:, 0:2, :])
-        nc.sync.dma_start(out=memory[2][:], in_=mem_rows[:, 2, :])
         nc.sync.dma_start(out=w_raw[1][:], in_=w_rows[:, 2:4, :])
         nc.sync.dma_start(out=x_table[:], in_=x_words[0].rearrange("p c r -> p (c r)").bitcast(I32))
-        nc.sync.dma_start(out=memory[LAST][:], in_=mem_rows[:, LAST, :])
-
-        nc.vector.tensor_copy(x_scale_picked[:], x_scale_table[:].indirect(token_list[:]))
-        for q in range(QUADRANTS):
-            nc.scalar.dma_start(
-                out=x_scale[32 * q : 32 * q + 4, :].bitcast(I32),
-                in_=x_scale_picked[scale_base + 4 * q : scale_base + 4 * q + 4, :].bitcast(I32),
-            )
 
         halves = [slice(h * S // 2, (h + 1) * S // 2) for h in range(2)]
         list_halves = [slice(h * S // LIST_ROWS // 2, (h + 1) * S // LIST_ROWS // 2) for h in range(2)]
 
-        def mean_of_slots(t, mean):
-            at_slot = keep.tile(
-                [P, S], F32, name="at_slot%d" % t, tag="w_grouped" if t == LAST else "at_slot%d" % t, align_bytes=64
+        at_slot = [keep.tile([P, S], F32, name="at_slot%d" % t, align_bytes=64) for t in range(PACK)]
+        at_from = [keep.tile([P, S], F32, name="at_from%d" % t, align_bytes=64) for t in range(PACK)]
+        means = {t: keep.tile([P, S], F32, name="mean%d" % t, align_bytes=64) for t in range(PACK)}
+        fresh = [keep.tile([P, S], F32, name="y%d" % t, align_bytes=64) for t in range(PACK)]
+
+        whole, whole_list = slice(0, S), slice(0, S // LIST_ROWS)
+
+        def look_up(t, cols, entries):
+            nc.scalar.activation(at_slot[t][:, cols], memory[t][:].indirect(slot_list[:, entries]), COPY, scale=0.5)
+            nc.scalar.activation(at_from[t][:, cols], memory[t][:].indirect(from_list[:, entries]), COPY, scale=0.5)
+            nc.vector.tensor_tensor(means[t][:, cols], at_slot[t][:, cols], at_from[t][:, cols], ADD)
+
+        nc.vector.tensor_copy(x_scale_picked[:], x_scale_table[:].indirect(token_list[:]))
+        nc.vector.tensor_scalar(at_slot[0][:], memory[0][:].indirect(slot_list[:]), 0.5, 0.0, MULT, ADD)
+        nc.scalar.activation(at_from[0][:], memory[0][:].indirect(from_list[:]), COPY, scale=0.5)
+        for q in range(QUADRANTS):
+            nc.sync.dma_start(
+                out=x_scale[32 * q : 32 * q + 4, :].bitcast(I32),
+                in_=x_scale_picked[scale_base + 4 * q : scale_base + 4 * q + 4, :].bitcast(I32),
             )
-            both = keep.tile([P, S], F32, name="both%d" % t, tag="x_table" if t == LAST else "both%d" % t, align_bytes=64)
-            for cols, entries in zip(halves, list_halves):
-                nc.vector.tensor_copy(at_slot[:, cols], memory[t][:].indirect(slot_list[:, entries]))
-            for cols, entries in zip(halves, list_halves):
-                nc.vector.tensor_tensor(both[:, cols], memory[t][:].indirect(from_list[:, entries]), at_slot[:, cols], ADD)
-            nc.scalar.activation(mean, both[:], COPY, scale=0.5)
 
         w_grouped = keep.tile([P, N * PACK], BF16, name="w_grouped", align_bytes=64)
         w_dealt = w_grouped[:].rearrange("p (t m j) -> p m t j", t=PACK, j=PACK)
-        for h in range(2):
-            nc.scalar.copy(
-                w_dealt[:, :, :, 2 * h : 2 * h + 2],
-                w_raw[h][:].rearrange("p j (m t) -> p m t j", t=PACK),
-            )
-
-        mean_pairs = [keep.tile([P, 2, S], F32, name="means%d" % h, tag="w_raw%d" % h, align_bytes=64) for h in range(2)]
-        means = [mean_pairs[0][:, 0, :], mean_pairs[1][:, 0, :], mean_pairs[1][:, 1, :], mean_pairs[0][:, 1, :]]
-        for t in range(LAST):
-            mean_of_slots(t, means[t])
+        w_read = [half[:].rearrange("p j (m t) -> p m t j", t=PACK) for half in w_raw]
+        nc.vector.tensor_tensor(means[0][:], at_slot[0][:], at_from[0][:], ADD)
+        nc.scalar.copy(w_dealt[:, :, :, 0:2], w_read[0])
+        nc.vector.tensor_copy(w_dealt[:, :W_VECTOR, :, 2:4], w_read[1][:, :W_VECTOR])
+        nc.scalar.copy(w_dealt[:, W_VECTOR:, :, 2:4], w_read[1][:, W_VECTOR:])
+        for t, tag in enumerate(("x_scale_table", "w_raw0", "w_raw1"), 1):
+            memory.append(keep.tile([P, U], F32, name="memory%d" % t, tag=tag, align_bytes=64))
+            nc.sync.dma_start(out=memory[t][:], in_=mem_rows[:, t, :])
 
         x_codes = keep.tile([P, S], U32, name="x_codes", align_bytes=64)
         w_codes = keep.tile([P, N], U32, name="w_codes", align_bytes=64)
         w_scale = keep.tile([P, N], U8, name="w_scale", align_bytes=64)
         nc.vector.quantize_mx(out=w_codes[:].bitcast(FP8X4), scales=w_scale[:], in_=w_grouped[:])
-        nc.vector.tensor_copy(x_codes[:], x_table[:].bitcast(U32).indirect(token_list[:]))
+        for cols, entries in zip(halves, list_halves):
+            nc.vector.tensor_copy(x_codes[:, cols], x_table[:].bitcast(U32).indirect(token_list[:, entries]))
 
-        fresh = {}
-        for t in range(PACK):
-            cols = slice(t * P, (t + 1) * P)
-            product = psum.tile([P, S], F32, name="product%d" % t)
+        def squash(t, h):
+            features, cols = slice(t * P, (t + 1) * P), halves[h]
+            product = psum.tile([P, S // 2], F32, name="first_product" if (t, h) == (0, 0) else "product")
             nc.tensor.matmul_mx(
                 out=product[:],
-                lhsT=w_codes[:, cols].bitcast(FP8X4),
-                lhsT_scale=w_scale[:, cols],
-                rhs=x_codes[:].bitcast(FP8X4),
-                rhs_scale=x_scale[:],
+                lhsT=w_codes[:, features].bitcast(FP8X4),
+                lhsT_scale=w_scale[:, features],
+                rhs=x_codes[:, cols].bitcast(FP8X4),
+                rhs_scale=x_scale[:, cols],
                 start=True,
                 stop=True,
             )
-            y = keep.tile([P, S], F32, name="y%d" % t, align_bytes=64)
-            nc.scalar.activation(y[:], product[:], TANH)
-            fresh[t] = y
+            nc.scalar.activation(fresh[t][:, cols], product[:], TANH)
 
+        def scatter(t, cols, entries):
+            nc.vector.tensor_tensor(memory[t][:].indirect(slot_list[:, entries]), fresh[t][:, cols], means[t][:, cols], ADD)
 
-        mean_of_slots(LAST, means[LAST])
+        squash(0, 0)
+        scatter(0, halves[0], list_halves[0])
+        squash(1, 0)
+        look_up(1, halves[0], list_halves[0])
+        squash(0, 1)
+        scatter(0, halves[1], list_halves[1])
+        nc.sync.dma_start(out=out_rows[:, 0, :], in_=memory[0][:])
+        look_up(1, halves[1], list_halves[1])
+        for t in range(1, LAST):
+            if t > 1:
+                squash(t, 0)
+            scatter(t, halves[0], list_halves[0])
+            look_up(t + 1, whole, whole_list)
+            squash(t, 1)
+            scatter(t, halves[1], list_halves[1])
+            nc.sync.dma_start(out=out_rows[:, t, :], in_=memory[t][:])
+        squash(LAST, 0)
+        squash(LAST, 1)
+        scatter(LAST, whole, whole_list)
+        nc.sync.dma_start(out=out_rows[:, LAST, :], in_=memory[LAST][:])
 
-        rounded = keep.tile(
-            [P, U * PACK], BF16, name="rounded", tag="x_codes", align_bytes=64
-        )
-        grouped = rounded[:].rearrange("p (c t) -> p c t", t=PACK)
+        pairs = [keep.tile([P, 2, b - a, 2], BF16, name="pairs%d" % a, align_bytes=64) for a, b in PIECES]
+        rounded = [keep.tile([P, (b - a) * PACK], BF16, name="rounded%d" % a, align_bytes=64) for a, b in PIECES]
+        out_codes = [keep.tile([P, b - a], I32, name="out_codes%d" % a, align_bytes=64) for a, b in STORES]
         out_scale = keep.tile([P, U], U8, name="out_scale", align_bytes=64)
         out_words = out_1[0].rearrange("p c r -> p (c r)").bitcast(I32)
-        out_codes = [
-            keep.tile([P, last - first], I32, name="out_codes%d" % first, align_bytes=64) for first, last in STORES
-        ]
+        for t in range(PACK):
+            for n, (a, b) in enumerate(PIECES):
+                nc.scalar.copy(pairs[n][:, t // 2, :, t % 2], memory[t][:, a:b])
 
-        def quantise(first, last):
-            n = [first >= a and last <= b for a, b in STORES].index(True)
-            a, b = STORES[n]
+        def weave(n, copy, dtype):
+            words = pairs[n][:].rearrange("p u c e -> p (u c e)").bitcast(dtype).rearrange("p (u c) -> p c u", u=2)
+            copy(rounded[n][:].bitcast(dtype).rearrange("p (c u) -> p c u", u=2), words)
+
+        def quantise(n):
+            first, last = PIECES[n]
+            m = [first >= a and last <= b for a, b in STORES].index(True)
+            a, b = STORES[m]
             nc.vector.quantize_mx(
-                out=out_codes[n][:, first - a : last - a].bitcast(FP8X4),
-                scales=out_scale[:, first:last],
-                in_=rounded[:, first * PACK : last * PACK],
+                out=out_codes[m][:, first - a : last - a].bitcast(FP8X4), scales=out_scale[:, first:last], in_=rounded[n][:]
             )
             if last == b:
-                nc.sync.dma_start(out=out_words[:, a:b], in_=out_codes[n][:])
+                nc.sync.dma_start(out=out_words[:, a:b], in_=out_codes[m][:])
 
-        for t in range(PACK):
-            nc.vector.tensor_tensor(memory[t][:].indirect(slot_list[:]), fresh[t][:], means[t], ADD)
-            nc.sync.dma_start(out=out_rows[:, t, :], in_=memory[t][:])
-            if t < 2:
-                nc.scalar.copy(grouped[:, :, t], memory[t][:])
-        nc.scalar.copy(
-            grouped[:, FILL:VECTOR_SHARE, 2:],
-            memory[2][:, FILL:VECTOR_SHARE].unsqueeze(2).to_broadcast([P, VECTOR_SHARE - FILL, 2]),
-        )
-        nc.scalar.copy(grouped[:, VECTOR_SHARE:, 2], memory[2][:, VECTOR_SHARE:])
-
-        nc.vector.tensor_copy(grouped[:, :FILL, 2], memory[2][:, :FILL])
-        for first, last in ((0, PIECE), (PIECE, VECTOR_SHARE)):
-            nc.vector.tensor_copy(grouped[:, first:last, LAST], memory[LAST][:, first:last])
-        for first, last in ((VECTOR_SHARE, 3 * PIECE), (3 * PIECE, LAST_HALF), (LAST_HALF, U)):
-            nc.scalar.copy(grouped[:, first:last, LAST], memory[LAST][:, first:last])
-        for first, last in QUANTISER_COLUMNS:
-            quantise(first, last)
+        by_vector = len(PIECES) - SCALAR_WEAVES
+        for n in range(by_vector, len(PIECES)):
+            weave(n, nc.scalar.copy, U32)
+        for n in range(by_vector):
+            weave(n, nc.vector.tensor_copy, I32)
+            if n > 0:
+                quantise(n - 1)
+        for n in range(by_vector - 1, len(PIECES)):
+            quantise(n)
         for q in range(QUADRANTS):
             queue = nc.scalar if q % 2 == 0 else nc.sync
             queue.dma_start(

@@ -21,8 +21,8 @@ P = 128
 PACK = 4
 LAST = PACK - 1
 LIST_ROWS = 16
-SCALE_ROWS = K // 32
 QUADRANTS = 4
+H = S // 2
 PIECES = ((0, 128), (128, 384), (384, 640), (640, 768), (768, 896), (896, U))
 STORES = ((0, 384), (384, 640), (640, 896), (896, U))
 SCALAR_WEAVES = 2
@@ -35,6 +35,7 @@ def tile_picked_slotadd_tanh_po_kernel(
     nc = tc.nc
     with ExitStack() as ctx:
         keep = ctx.enter_context(tc.tile_pool(name="keep", bufs=1))
+        shared = ctx.enter_context(tc.tile_pool(name="shared", bufs=1))
         psum = ctx.enter_context(tc.psum_pool(name="psum", bufs=1))
 
         mem_rows = mem.rearrange("(p t) c -> p t c", t=PACK)
@@ -49,7 +50,7 @@ def tile_picked_slotadd_tanh_po_kernel(
         x_table = keep.tile([P, T], I32, name="x_table", align_bytes=64)
         x_scale_table = keep.tile([P, T], U8, name="x_scale_table", align_bytes=64)
 
-        scale_base = P - SCALE_ROWS
+        scale_base = P - K // 32
         x_scale_picked = keep.tile([P, S], U8, name="x_scale_picked", align_bytes=64)
         x_scale = keep.tile([P, S], U8, name="x_scale", align_bytes=64)
         nc.scalar.dma_start(out=x_scale_table[scale_base:, :].bitcast(I32), in_=x_scales[0].bitcast(I32))
@@ -67,24 +68,21 @@ def tile_picked_slotadd_tanh_po_kernel(
         nc.sync.dma_start(out=w_raw[1][:], in_=w_rows[:, 2:4, :])
         nc.sync.dma_start(out=x_table[:], in_=x_words[0].rearrange("p c r -> p (c r)").bitcast(I32))
 
-        halves = [slice(h * S // 2, (h + 1) * S // 2) for h in range(2)]
-        list_halves = [slice(h * S // LIST_ROWS // 2, (h + 1) * S // LIST_ROWS // 2) for h in range(2)]
+        def entries(first, last):
+            return slice(first // LIST_ROWS, last // LIST_ROWS)
 
-        at_slot = [keep.tile([P, S], F32, name="at_slot%d" % t, align_bytes=64) for t in range(PACK)]
-        at_from = [keep.tile([P, S], F32, name="at_from%d" % t, align_bytes=64) for t in range(PACK)]
-        means = {t: keep.tile([P, S], F32, name="mean%d" % t, align_bytes=64) for t in range(PACK)}
-        fresh = [keep.tile([P, S], F32, name="y%d" % t, align_bytes=64) for t in range(PACK)]
+        def look_up(out, t, places, first, last):
+            nc.scalar.activation(out, memory[t][:].indirect(places[:, entries(first, last)]), COPY, scale=0.5)
 
-        whole, whole_list = slice(0, S), slice(0, S // LIST_ROWS)
+        def values(name, width, tag=None):
+            return keep.tile([P, width], F32, name=name, tag=tag or name, align_bytes=64)
 
-        def look_up(t, cols, entries):
-            nc.scalar.activation(at_slot[t][:, cols], memory[t][:].indirect(slot_list[:, entries]), COPY, scale=0.5)
-            nc.scalar.activation(at_from[t][:, cols], memory[t][:].indirect(from_list[:, entries]), COPY, scale=0.5)
-            nc.vector.tensor_tensor(means[t][:, cols], at_slot[t][:, cols], at_from[t][:, cols], ADD)
+        at_slot0, at_from0 = values("at_slot0", S), values("at_from0", S)
+        addends = values("addends", S + H)
 
         nc.vector.tensor_copy(x_scale_picked[:], x_scale_table[:].indirect(token_list[:]))
-        nc.vector.tensor_scalar(at_slot[0][:], memory[0][:].indirect(slot_list[:]), 0.5, 0.0, MULT, ADD)
-        nc.scalar.activation(at_from[0][:], memory[0][:].indirect(from_list[:]), COPY, scale=0.5)
+        nc.vector.tensor_scalar(at_slot0[:], memory[0][:].indirect(slot_list[:]), 0.5, 0.0, MULT, ADD)
+        look_up(at_from0[:], 0, from_list, 0, S)
         for q in range(QUADRANTS):
             nc.sync.dma_start(
                 out=x_scale[32 * q : 32 * q + 4, :].bitcast(I32),
@@ -94,10 +92,11 @@ def tile_picked_slotadd_tanh_po_kernel(
         w_grouped = keep.tile([P, N * PACK], BF16, name="w_grouped", align_bytes=64)
         w_dealt = w_grouped[:].rearrange("p (t m j) -> p m t j", t=PACK, j=PACK)
         w_read = [half[:].rearrange("p j (m t) -> p m t j", t=PACK) for half in w_raw]
-        nc.vector.tensor_tensor(means[0][:], at_slot[0][:], at_from[0][:], ADD)
+        nc.vector.tensor_tensor(addends[:, :S], at_slot0[:], at_from0[:], ADD)
         nc.scalar.copy(w_dealt[:, :, :, 0:2], w_read[0])
         nc.vector.tensor_copy(w_dealt[:, :W_VECTOR, :, 2:4], w_read[1][:, :W_VECTOR])
         nc.scalar.copy(w_dealt[:, W_VECTOR:, :, 2:4], w_read[1][:, W_VECTOR:])
+
         for t, tag in enumerate(("x_scale_table", "w_raw0", "w_raw1"), 1):
             memory.append(keep.tile([P, U], F32, name="memory%d" % t, tag=tag, align_bytes=64))
             nc.sync.dma_start(out=memory[t][:], in_=mem_rows[:, t, :])
@@ -106,48 +105,89 @@ def tile_picked_slotadd_tanh_po_kernel(
         w_codes = keep.tile([P, N], U32, name="w_codes", align_bytes=64)
         w_scale = keep.tile([P, N], U8, name="w_scale", align_bytes=64)
         nc.vector.quantize_mx(out=w_codes[:].bitcast(FP8X4), scales=w_scale[:], in_=w_grouped[:])
-        for cols, entries in zip(halves, list_halves):
-            nc.vector.tensor_copy(x_codes[:, cols], x_table[:].bitcast(U32).indirect(token_list[:, entries]))
-
-        def squash(t, h):
-            features, cols = slice(t * P, (t + 1) * P), halves[h]
-            product = psum.tile([P, S // 2], F32, name="first_product" if (t, h) == (0, 0) else "product")
-            nc.tensor.matmul_mx(
-                out=product[:],
-                lhsT=w_codes[:, features].bitcast(FP8X4),
-                lhsT_scale=w_scale[:, features],
-                rhs=x_codes[:, cols].bitcast(FP8X4),
-                rhs_scale=x_scale[:, cols],
-                start=True,
-                stop=True,
+        for first in (0, H):
+            nc.vector.tensor_copy(
+                x_codes[:, first : first + H], x_table[:].bitcast(U32).indirect(token_list[:, entries(first, first + H)])
             )
-            nc.scalar.activation(fresh[t][:, cols], product[:], TANH)
 
-        def scatter(t, cols, entries):
-            nc.vector.tensor_tensor(memory[t][:].indirect(slot_list[:, entries]), fresh[t][:, cols], means[t][:, cols], ADD)
+        def squash(name, parts, tag=None):
+            width = sum(last - first for t, first, last in parts)
+            product = psum.tile([P, width], F32, name="product_" + name)
+            fresh = values("fresh_" + name, width, tag)
+            at = 0
+            for t, first, last in parts:
+                features = slice(t * P, (t + 1) * P)
+                nc.tensor.matmul_mx(
+                    out=product[:, at : at + last - first],
+                    lhsT=w_codes[:, features].bitcast(FP8X4),
+                    lhsT_scale=w_scale[:, features],
+                    rhs=x_codes[:, first:last].bitcast(FP8X4),
+                    rhs_scale=x_scale[:, first:last],
+                    start=True,
+                    stop=True,
+                )
+                at = at + last - first
+            nc.scalar.activation(fresh[:], product[:], TANH)
+            return fresh
 
-        squash(0, 0)
-        scatter(0, halves[0], list_halves[0])
-        squash(1, 0)
-        look_up(1, halves[0], list_halves[0])
-        squash(0, 1)
-        scatter(0, halves[1], list_halves[1])
+        def window(t, first, last):
+            return memory[t][:].indirect(slot_list[:, entries(first, last)])
+
+        def scatter(t, first, last, update):
+            nc.vector.tensor_copy(window(t, first, last), update)
+
+        def add(name, width, a, b, tag=None):
+            total = values(name, width, tag)
+            nc.gpsimd.tensor_tensor(total[:], a, b, ADD)
+            return total
+
+        def fetch(name, t, places, first, last):
+            found = values(name, last - first)
+            look_up(found[:], t, places, first, last)
+            return found
+
+        y = squash("0a", [(0, 0, H)])
+        nc.vector.tensor_tensor(window(0, 0, H), y[:], addends[:, :H], ADD)
+        look_up(addends[:, S:], 1, slot_list, 0, H)
+        y = squash("0b1a", [(0, H, S), (1, 0, H)])
+        mixed = values("mixed", S)
+        nc.vector.tensor_tensor(mixed[:], y[:], addends[:, H:], ADD)
+        scatter(0, H, S, mixed[:, :H])
         nc.sync.dma_start(out=out_rows[:, 0, :], in_=memory[0][:])
-        look_up(1, halves[1], list_halves[1])
-        for t in range(1, LAST):
-            if t > 1:
-                squash(t, 0)
-            scatter(t, halves[0], list_halves[0])
-            look_up(t + 1, whole, whole_list)
-            squash(t, 1)
-            scatter(t, halves[1], list_halves[1])
-            nc.sync.dma_start(out=out_rows[:, t, :], in_=memory[t][:])
-        squash(LAST, 0)
-        squash(LAST, 1)
-        scatter(LAST, whole, whole_list)
+        at_from = fetch("at_from1a", 1, from_list, 0, H)
+        update_a = add("update1a", H, mixed[:, H:], at_from[:])
+        at_slot = fetch("at_slot1b", 1, slot_list, H, S)
+        y = squash("1b", [(1, H, S)], "fresh_0b1a")
+        partial = add("partial1b", H, y[:], at_slot[:])
+        at_from = fetch("at_from1b", 1, from_list, H, S)
+        update_b = add("update1b", H, partial[:], at_from[:])
+        scatter(1, 0, H, update_a[:])
+        scatter(1, H, S, update_b[:])
+        nc.sync.dma_start(out=out_rows[:, 1, :], in_=memory[1][:])
+
+        at_slot = fetch("at_slot2", 2, slot_list, 0, S)
+        y = squash("2", [(2, 0, S)], "addends")
+        partial = add("partial2", S, y[:], at_slot[:], "at_from1b")
+        at_from = fetch("at_from2", 2, from_list, 0, S)
+        for first in (0, H):
+            cols = slice(first, first + H)
+            update = add("update2_%d" % first, H, partial[:, cols], at_from[:, cols])
+            scatter(2, first, first + H, update[:])
+        nc.sync.dma_start(out=out_rows[:, 2, :], in_=memory[2][:])
+
+        at_slot = shared.tile([P, 3 * S], F32, name="at_slot3", offset=1024, align_bytes=64)
+        look_up(at_slot[:, :S], LAST, slot_list, 0, S)
+        y = squash("3", [(LAST, 0, S)], "at_from1a")
+        partial = add("partial3", S, y[:], at_slot[:, :S], "at_from2")
+        at_from = fetch("at_from3", LAST, from_list, 0, S)
+        update = add("update3", S, partial[:], at_from[:])
+        scatter(LAST, 0, S, update[:])
         nc.sync.dma_start(out=out_rows[:, LAST, :], in_=memory[LAST][:])
 
-        pairs = [keep.tile([P, 2, b - a, 2], BF16, name="pairs%d" % a, align_bytes=64) for a, b in PIECES]
+        places = (2048, 0, 6144, 3072, 4096, 5120)
+        pairs = [
+            shared.tile([P, 2, b - a, 2], BF16, name="pairs%d" % a, offset=at, align_bytes=64) for (a, b), at in zip(PIECES, places)
+        ]
         rounded = [keep.tile([P, (b - a) * PACK], BF16, name="rounded%d" % a, align_bytes=64) for a, b in PIECES]
         out_codes = [keep.tile([P, b - a], I32, name="out_codes%d" % a, align_bytes=64) for a, b in STORES]
         out_scale = keep.tile([P, U], U8, name="out_scale", align_bytes=64)

@@ -21,12 +21,12 @@ P = 128
 PACK = 4
 LAST = PACK - 1
 LIST_ROWS = 16
+SCALE_ROWS = K // 32
 QUADRANTS = 4
-H = S // 2
-PIECES = ((0, 128), (128, 384), (384, 640), (640, 768), (768, 896), (896, U))
-STORES = ((0, 384), (384, 640), (640, 896), (896, U))
-SCALAR_WEAVES = 2
-W_VECTOR = 80
+PIECES = ((0, 128), (128, 256), (256, 512), (512, 768), (768, U))
+STORES = ((0, 256), (256, 512), (512, 768), (768, U))
+SCALAR_WEAVES = 1
+W_VECTOR = 112
 
 
 def tile_picked_slotadd_tanh_po_kernel(
@@ -45,12 +45,12 @@ def tile_picked_slotadd_tanh_po_kernel(
         slot_list = keep.tile([P, S // LIST_ROWS], U16, name="slot_list")
         from_list = keep.tile([P, S // LIST_ROWS], U16, name="from_list")
         token_list = keep.tile([P, S // LIST_ROWS], U16, name="token_list")
-        memory = [keep.tile([P, U], F32, name="memory0", align_bytes=64)]
+        memory = [keep.tile([P, U], F32, name="memory%d" % t, align_bytes=64) for t in range(2)]
         w_raw = [keep.tile([P, PACK // 2, N], F32, name="w_raw%d" % h, align_bytes=64) for h in range(2)]
         x_table = keep.tile([P, T], I32, name="x_table", align_bytes=64)
         x_scale_table = keep.tile([P, T], U8, name="x_scale_table", align_bytes=64)
 
-        scale_base = P - K // 32
+        scale_base = P - SCALE_ROWS
         x_scale_picked = keep.tile([P, S], U8, name="x_scale_picked", align_bytes=64)
         x_scale = keep.tile([P, S], U8, name="x_scale", align_bytes=64)
         nc.scalar.dma_start(out=x_scale_table[scale_base:, :].bitcast(I32), in_=x_scales[0].bitcast(I32))
@@ -66,135 +66,127 @@ def tile_picked_slotadd_tanh_po_kernel(
         nc.sync.dma_start(from_list[:], from_l)
         nc.sync.dma_start(out=w_raw[0][:], in_=w_rows[:, 0:2, :])
         nc.sync.dma_start(out=w_raw[1][:], in_=w_rows[:, 2:4, :])
+        nc.sync.dma_start(out=memory[1][:], in_=mem_rows[:, 1, :])
         nc.sync.dma_start(out=x_table[:], in_=x_words[0].rearrange("p c r -> p (c r)").bitcast(I32))
 
-        def entries(first, last):
-            return slice(first // LIST_ROWS, last // LIST_ROWS)
+        halves = [slice(h * S // 2, (h + 1) * S // 2) for h in range(2)]
+        list_halves = [slice(h * S // LIST_ROWS // 2, (h + 1) * S // LIST_ROWS // 2) for h in range(2)]
 
-        def look_up(out, t, places, first, last):
-            nc.scalar.activation(out, memory[t][:].indirect(places[:, entries(first, last)]), COPY, scale=0.5)
+        at_slot = [keep.tile([P, S], F32, name="at_slot%d" % t, align_bytes=64) for t in range(PACK)]
+        at_from = [keep.tile([P, S], F32, name="at_from%d" % t, align_bytes=64) for t in range(PACK)]
+        means = [keep.tile([P, S], F32, name="mean%d" % t, align_bytes=64) for t in range(2)]
+        whole = slice(0, S)
 
         def values(name, width, tag=None):
             return keep.tile([P, width], F32, name=name, tag=tag or name, align_bytes=64)
 
-        at_slot0, at_from0 = values("at_slot0", S), values("at_from0", S)
-        addends = values("addends", S + H)
+        def look_up(out, t, places):
+            nc.scalar.activation(out, memory[t][:].indirect(places[:]), COPY, scale=0.5)
 
         nc.vector.tensor_copy(x_scale_picked[:], x_scale_table[:].indirect(token_list[:]))
-        nc.vector.tensor_scalar(at_slot0[:], memory[0][:].indirect(slot_list[:]), 0.5, 0.0, MULT, ADD)
-        look_up(at_from0[:], 0, from_list, 0, S)
-        for q in range(QUADRANTS):
+        nc.vector.tensor_scalar(at_slot[0][:], memory[0][:].indirect(slot_list[:]), 0.5, 0.0, MULT, ADD)
+        nc.scalar.activation(at_from[0][:], memory[0][:].indirect(from_list[:]), COPY, scale=0.5)
+
+        def move_scales(q, cols):
             nc.sync.dma_start(
-                out=x_scale[32 * q : 32 * q + 4, :].bitcast(I32),
-                in_=x_scale_picked[scale_base + 4 * q : scale_base + 4 * q + 4, :].bitcast(I32),
+                out=x_scale[32 * q : 32 * q + 4, cols].bitcast(I32),
+                in_=x_scale_picked[scale_base + 4 * q : scale_base + 4 * q + 4, cols].bitcast(I32),
             )
+
+        for q in range(QUADRANTS):
+            move_scales(q, whole)
 
         w_grouped = keep.tile([P, N * PACK], BF16, name="w_grouped", align_bytes=64)
         w_dealt = w_grouped[:].rearrange("p (t m j) -> p m t j", t=PACK, j=PACK)
         w_read = [half[:].rearrange("p j (m t) -> p m t j", t=PACK) for half in w_raw]
-        nc.vector.tensor_tensor(addends[:, :S], at_slot0[:], at_from0[:], ADD)
+        nc.vector.tensor_tensor(means[0][:], at_slot[0][:], at_from[0][:], ADD)
         nc.scalar.copy(w_dealt[:, :, :, 0:2], w_read[0])
         nc.vector.tensor_copy(w_dealt[:, :W_VECTOR, :, 2:4], w_read[1][:, :W_VECTOR])
         nc.scalar.copy(w_dealt[:, W_VECTOR:, :, 2:4], w_read[1][:, W_VECTOR:])
-
-        for t, tag in enumerate(("x_scale_table", "w_raw0", "w_raw1"), 1):
+        for t, tag in enumerate(("x_scale_table", "w_raw0"), 2):
             memory.append(keep.tile([P, U], F32, name="memory%d" % t, tag=tag, align_bytes=64))
             nc.sync.dma_start(out=memory[t][:], in_=mem_rows[:, t, :])
 
         x_codes = keep.tile([P, S], U32, name="x_codes", align_bytes=64)
-        w_codes = keep.tile([P, N], U32, name="w_codes", align_bytes=64)
+        w_codes = [
+            keep.tile([P, N // 2], U32, name="w_codes0", align_bytes=64),
+            keep.tile([P, N // 2], U32, name="w_codes1", align_bytes=64),
+        ]
         w_scale = keep.tile([P, N], U8, name="w_scale", align_bytes=64)
-        nc.vector.quantize_mx(out=w_codes[:].bitcast(FP8X4), scales=w_scale[:], in_=w_grouped[:])
-        for first in (0, H):
+        for u in range(2):
+            nc.vector.quantize_mx(
+                out=w_codes[u][:].bitcast(FP8X4),
+                scales=w_scale[:, u * N // 2 : (u + 1) * N // 2],
+                in_=w_grouped[:, u * N * PACK // 2 : (u + 1) * N * PACK // 2],
+            )
+        nc.vector.tensor_scalar(at_slot[1][:], memory[1][:].indirect(slot_list[:]), 0.5, 0.0, MULT, ADD)
+        look_up(at_from[1][:], 1, from_list)
+        nc.gpsimd.tensor_tensor(means[1][:], at_slot[1][:], at_from[1][:], ADD)
+        for first, last in ((0, S // 4), (S // 4, S // 2), (S // 2, S)):
             nc.vector.tensor_copy(
-                x_codes[:, first : first + H], x_table[:].bitcast(U32).indirect(token_list[:, entries(first, first + H)])
+                x_codes[:, first:last], x_table[:].bitcast(U32).indirect(token_list[:, first // LIST_ROWS : last // LIST_ROWS])
             )
 
-        def squash(name, parts, tag=None):
-            width = sum(last - first for t, first, last in parts)
-            product = psum.tile([P, width], F32, name="product_" + name)
-            fresh = values("fresh_" + name, width, tag)
-            at = 0
-            for t, first, last in parts:
-                features = slice(t * P, (t + 1) * P)
-                nc.tensor.matmul_mx(
-                    out=product[:, at : at + last - first],
-                    lhsT=w_codes[:, features].bitcast(FP8X4),
-                    lhsT_scale=w_scale[:, features],
-                    rhs=x_codes[:, first:last].bitcast(FP8X4),
-                    rhs_scale=x_scale[:, first:last],
-                    start=True,
-                    stop=True,
-                )
-                at = at + last - first
-            nc.scalar.activation(fresh[:], product[:], TANH)
-            return fresh
+        quarters = [slice(0, S // 4), slice(S // 4, S // 2)]
+        parts = [(0, quarters[0]), (0, quarters[1]), (1, whole), (0, halves[1]), (2, whole), (LAST, whole)]
+        products = {}
+        for t, cols in parts:
+            features = slice(t * P, (t + 1) * P)
+            product = psum.tile([P, cols.stop - cols.start], F32, name="product%d_%d" % (t, cols.start))
+            nc.tensor.matmul_mx(
+                out=product[:],
+                lhsT=w_codes[t // 2][:, t % 2 * P : (t % 2 + 1) * P].bitcast(FP8X4),
+                lhsT_scale=w_scale[:, features],
+                rhs=x_codes[:, cols].bitcast(FP8X4),
+                rhs_scale=x_scale[:, cols],
+                start=True,
+                stop=True,
+            )
+            products[t, cols.start] = product
 
-        def window(t, first, last):
-            return memory[t][:].indirect(slot_list[:, entries(first, last)])
+        def squash(t, first, out):
+            nc.scalar.activation(out, products[t, first][:], TANH)
 
-        def scatter(t, first, last, update):
-            nc.vector.tensor_copy(window(t, first, last), update)
-
-        def add(name, width, a, b, tag=None):
-            total = values(name, width, tag)
-            nc.gpsimd.tensor_tensor(total[:], a, b, ADD)
-            return total
-
-        def fetch(name, t, places, first, last):
-            found = values(name, last - first)
-            look_up(found[:], t, places, first, last)
-            return found
-
-        y = squash("0a", [(0, 0, H)])
-        nc.vector.tensor_tensor(window(0, 0, H), y[:], addends[:, :H], ADD)
-        look_up(addends[:, S:], 1, slot_list, 0, H)
-        y = squash("0b1a", [(0, H, S), (1, 0, H)])
-        mixed = values("mixed", S)
-        nc.vector.tensor_tensor(mixed[:], y[:], addends[:, H:], ADD)
-        scatter(0, H, S, mixed[:, :H])
+        fresh = [values("y0_%d" % h, S // 2) for h in range(2)]
+        for cols in quarters:
+            squash(0, cols.start, fresh[0][:, cols])
+        nc.vector.tensor_tensor(memory[0][:].indirect(slot_list[:, list_halves[0]]), fresh[0][:], means[0][:, halves[0]], ADD)
+        y = values("y1", S)
+        squash(1, 0, y[:])
+        update = values("update1", S)
+        nc.vector.tensor_tensor(update[:], y[:], means[1][:], ADD)
+        squash(0, S // 2, fresh[1][:])
+        nc.vector.tensor_tensor(memory[0][:].indirect(slot_list[:, list_halves[1]]), fresh[1][:], means[0][:, halves[1]], ADD)
         nc.sync.dma_start(out=out_rows[:, 0, :], in_=memory[0][:])
-        at_from = fetch("at_from1a", 1, from_list, 0, H)
-        update_a = add("update1a", H, mixed[:, H:], at_from[:])
-        at_slot = fetch("at_slot1b", 1, slot_list, H, S)
-        y = squash("1b", [(1, H, S)], "fresh_0b1a")
-        partial = add("partial1b", H, y[:], at_slot[:])
-        at_from = fetch("at_from1b", 1, from_list, H, S)
-        update_b = add("update1b", H, partial[:], at_from[:])
-        scatter(1, 0, H, update_a[:])
-        scatter(1, H, S, update_b[:])
+        nc.vector.tensor_copy(memory[1][:].indirect(slot_list[:]), update[:])
         nc.sync.dma_start(out=out_rows[:, 1, :], in_=memory[1][:])
+        at_from[2] = shared.tile([P, 3 * S], F32, name="from2", offset=2048, align_bytes=64)
+        for t in range(2, PACK):
+            y = values("y%d" % t, S)
+            squash(t, 0, y[:])
+            look_up(at_slot[t][:], t, slot_list)
+            partial = values("partial%d" % t, S, "y0_1")
+            nc.gpsimd.tensor_tensor(partial[:], y[:], at_slot[t][:], ADD)
+            look_up(at_from[t][:, :S], t, from_list)
+            update = values("update%d" % t, S)
+            nc.gpsimd.tensor_tensor(update[:], partial[:], at_from[t][:, :S], ADD)
+            nc.vector.tensor_copy(memory[t][:].indirect(slot_list[:]), update[:])
+            nc.sync.dma_start(out=out_rows[:, t, :], in_=memory[t][:])
 
-        at_slot = fetch("at_slot2", 2, slot_list, 0, S)
-        y = squash("2", [(2, 0, S)], "addends")
-        partial = add("partial2", S, y[:], at_slot[:], "at_from1b")
-        at_from = fetch("at_from2", 2, from_list, 0, S)
-        for first in (0, H):
-            cols = slice(first, first + H)
-            update = add("update2_%d" % first, H, partial[:, cols], at_from[:, cols])
-            scatter(2, first, first + H, update[:])
-        nc.sync.dma_start(out=out_rows[:, 2, :], in_=memory[2][:])
-
-        at_slot = shared.tile([P, 3 * S], F32, name="at_slot3", offset=1024, align_bytes=64)
-        look_up(at_slot[:, :S], LAST, slot_list, 0, S)
-        y = squash("3", [(LAST, 0, S)], "at_from1a")
-        partial = add("partial3", S, y[:], at_slot[:, :S], "at_from2")
-        at_from = fetch("at_from3", LAST, from_list, 0, S)
-        update = add("update3", S, partial[:], at_from[:])
-        scatter(LAST, 0, S, update[:])
-        nc.sync.dma_start(out=out_rows[:, LAST, :], in_=memory[LAST][:])
-
-        places = (2048, 0, 6144, 3072, 4096, 5120)
+        places = (3072, 4096, 1024, 5120)
         pairs = [
             shared.tile([P, 2, b - a, 2], BF16, name="pairs%d" % a, offset=at, align_bytes=64) for (a, b), at in zip(PIECES, places)
         ]
+        pairs.append(keep.tile([P, 2, U - PIECES[-1][0], 2], BF16, name="last_pairs", tag="at_from3", align_bytes=64))
         rounded = [keep.tile([P, (b - a) * PACK], BF16, name="rounded%d" % a, align_bytes=64) for a, b in PIECES]
         out_codes = [keep.tile([P, b - a], I32, name="out_codes%d" % a, align_bytes=64) for a, b in STORES]
         out_scale = keep.tile([P, U], U8, name="out_scale", align_bytes=64)
         out_words = out_1[0].rearrange("p c r -> p (c r)").bitcast(I32)
+        by_vector = len(PIECES) - SCALAR_WEAVES
         for t in range(PACK):
             for n, (a, b) in enumerate(PIECES):
-                nc.scalar.copy(pairs[n][:, t // 2, :, t % 2], memory[t][:, a:b])
+                copy = nc.vector.tensor_copy if t >= 2 and n >= by_vector else nc.scalar.copy
+                copy(pairs[n][:, t // 2, :, t % 2], memory[t][:, a:b])
 
         def weave(n, copy, dtype):
             words = pairs[n][:].rearrange("p u c e -> p (u c e)").bitcast(dtype).rearrange("p (u c) -> p c u", u=2)
@@ -210,7 +202,6 @@ def tile_picked_slotadd_tanh_po_kernel(
             if last == b:
                 nc.sync.dma_start(out=out_words[:, a:b], in_=out_codes[m][:])
 
-        by_vector = len(PIECES) - SCALAR_WEAVES
         for n in range(by_vector, len(PIECES)):
             weave(n, nc.scalar.copy, U32)
         for n in range(by_vector):

@@ -74,6 +74,7 @@ def tile_picked_slotadd_tanh_po_kernel(
 
         at_slot = [keep.tile([P, S], F32, name="at_slot%d" % t, align_bytes=64) for t in range(PACK)]
         at_from = [keep.tile([P, S], F32, name="at_from%d" % t, align_bytes=64) for t in range(PACK)]
+        first_mean = shared.tile([P, S // 2], F32, name="first_mean", offset=11264, align_bytes=64)
         means = [keep.tile([P, S], F32, name="mean%d" % t, align_bytes=64) for t in range(2)]
         whole = slice(0, S)
 
@@ -99,7 +100,8 @@ def tile_picked_slotadd_tanh_po_kernel(
         w_grouped = keep.tile([P, N * PACK], BF16, name="w_grouped", align_bytes=64)
         w_dealt = w_grouped[:].rearrange("p (t m j) -> p m t j", t=PACK, j=PACK)
         w_read = [half[:].rearrange("p j (m t) -> p m t j", t=PACK) for half in w_raw]
-        nc.vector.tensor_tensor(means[0][:], at_slot[0][:], at_from[0][:], ADD)
+        nc.vector.tensor_tensor(first_mean[:], at_slot[0][:, halves[0]], at_from[0][:, halves[0]], ADD)
+        nc.vector.tensor_tensor(means[0][:, halves[1]], at_slot[0][:, halves[1]], at_from[0][:, halves[1]], ADD)
         nc.scalar.copy(w_dealt[:, :, :, 0:2], w_read[0])
         nc.vector.tensor_copy(w_dealt[:, :W_VECTOR, :, 2:4], w_read[1][:, :W_VECTOR])
         nc.scalar.copy(w_dealt[:, W_VECTOR:, :, 2:4], w_read[1][:, W_VECTOR:])
@@ -128,44 +130,55 @@ def tile_picked_slotadd_tanh_po_kernel(
             )
 
         quarters = [slice(0, S // 4), slice(S // 4, S // 2)]
-        parts = [(0, quarters[0]), (0, quarters[1]), (1, whole), (0, halves[1]), (2, whole), (LAST, whole)]
+        parts = [(t, [cols]) for cols in quarters for t in (1, 0)]
+        parts = parts + [(0, [halves[1]]), (1, [halves[1]]), (2, [whole]), (LAST, [whole])]
         products = {}
-        for t, cols in parts:
+        for t, passes in parts:
             features = slice(t * P, (t + 1) * P)
-            product = psum.tile([P, cols.stop - cols.start], F32, name="product%d_%d" % (t, cols.start))
-            nc.tensor.matmul_mx(
-                out=product[:],
-                lhsT=w_codes[t // 2][:, t % 2 * P : (t % 2 + 1) * P].bitcast(FP8X4),
-                lhsT_scale=w_scale[:, features],
-                rhs=x_codes[:, cols].bitcast(FP8X4),
-                rhs_scale=x_scale[:, cols],
-                start=True,
-                stop=True,
-            )
-            products[t, cols.start] = product
+            first = passes[0].start
+            product = psum.tile([P, passes[-1].stop - first], F32, name="product%d_%d" % (t, first))
+            for cols in passes:
+                nc.tensor.matmul_mx(
+                    out=product[:, cols.start - first : cols.stop - first],
+                    lhsT=w_codes[t // 2][:, t % 2 * P : (t % 2 + 1) * P].bitcast(FP8X4),
+                    lhsT_scale=w_scale[:, features],
+                    rhs=x_codes[:, cols].bitcast(FP8X4),
+                    rhs_scale=x_scale[:, cols],
+                    start=True,
+                    stop=True,
+                )
+            products[t, first] = product
 
         def squash(t, first, out):
             nc.scalar.activation(out, products[t, first][:], TANH)
 
-        fresh = [values("y0_%d" % h, S // 2) for h in range(2)]
+        def scatter(t, h, update):
+            nc.vector.tensor_copy(memory[t][:].indirect(slot_list[:, list_halves[h]]), update[:])
+
+        early, y = values("y1_0", S // 2), values("y0_0", S // 2)
+        update = values("update1_0", S // 2)
         for cols in quarters:
-            squash(0, cols.start, fresh[0][:, cols])
-        nc.vector.tensor_tensor(memory[0][:].indirect(slot_list[:, list_halves[0]]), fresh[0][:], means[0][:, halves[0]], ADD)
-        y = values("y1", S)
-        squash(1, 0, y[:])
-        update = values("update1", S)
-        nc.vector.tensor_tensor(update[:], y[:], means[1][:], ADD)
-        squash(0, S // 2, fresh[1][:])
-        nc.vector.tensor_tensor(memory[0][:].indirect(slot_list[:, list_halves[1]]), fresh[1][:], means[0][:, halves[1]], ADD)
-        nc.sync.dma_start(out=out_rows[:, 0, :], in_=memory[0][:])
-        nc.vector.tensor_copy(memory[1][:].indirect(slot_list[:]), update[:])
-        nc.sync.dma_start(out=out_rows[:, 1, :], in_=memory[1][:])
+            squash(1, cols.start, early[:, cols])
+            nc.vector.tensor_tensor(update[:, cols], early[:, cols], means[1][:, cols], ADD)
+            squash(0, cols.start, y[:, cols])
+        nc.vector.tensor_tensor(memory[0][:].indirect(slot_list[:, list_halves[0]]), y[:], first_mean[:], ADD)
+        scatter(1, 0, update)
+        for t in range(2):
+            y = values("y%d_1" % t, S // 2)
+            squash(t, S // 2, y[:])
+            if t == 0:
+                update = values("update0_1", S // 2, "y0_0")
+            else:
+                update = shared.tile([P, S // 2], F32, name="update1_1", offset=10752, align_bytes=64)
+            nc.gpsimd.tensor_tensor(update[:], y[:], means[t][:, halves[1]], ADD)
+            scatter(t, 1, update)
+            nc.sync.dma_start(out=out_rows[:, t, :], in_=memory[t][:])
         at_from[2] = shared.tile([P, 3 * S], F32, name="from2", offset=2048, align_bytes=64)
         for t in range(2, PACK):
             y = values("y%d" % t, S)
             squash(t, 0, y[:])
             look_up(at_slot[t][:], t, slot_list)
-            partial = values("partial%d" % t, S, "y0_1")
+            partial = shared.tile([P, S], F32, name="partial%d" % t, offset=11776, align_bytes=64)
             nc.gpsimd.tensor_tensor(partial[:], y[:], at_slot[t][:], ADD)
             look_up(at_from[t][:, :S], t, from_list)
             update = values("update%d" % t, S)

@@ -74,7 +74,6 @@ def tile_picked_slotadd_tanh_po_kernel(
 
         at_slot = [keep.tile([P, S], F32, name="at_slot%d" % t, align_bytes=64) for t in range(PACK)]
         at_from = [keep.tile([P, S], F32, name="at_from%d" % t, align_bytes=64) for t in range(PACK)]
-        first_mean = shared.tile([P, S // 2], F32, name="first_mean", offset=11264, align_bytes=64)
         means = [keep.tile([P, S], F32, name="mean%d" % t, align_bytes=64) for t in range(2)]
         whole = slice(0, S)
 
@@ -100,8 +99,7 @@ def tile_picked_slotadd_tanh_po_kernel(
         w_grouped = keep.tile([P, N * PACK], BF16, name="w_grouped", align_bytes=64)
         w_dealt = w_grouped[:].rearrange("p (t m j) -> p m t j", t=PACK, j=PACK)
         w_read = [half[:].rearrange("p j (m t) -> p m t j", t=PACK) for half in w_raw]
-        nc.vector.tensor_tensor(first_mean[:], at_slot[0][:, halves[0]], at_from[0][:, halves[0]], ADD)
-        nc.vector.tensor_tensor(means[0][:, halves[1]], at_slot[0][:, halves[1]], at_from[0][:, halves[1]], ADD)
+        nc.vector.tensor_tensor(means[0][:], at_slot[0][:], at_from[0][:], ADD)
         nc.scalar.copy(w_dealt[:, :, :, 0:2], w_read[0])
         nc.vector.tensor_copy(w_dealt[:, :W_VECTOR, :, 2:4], w_read[1][:, :W_VECTOR])
         nc.scalar.copy(w_dealt[:, W_VECTOR:, :, 2:4], w_read[1][:, W_VECTOR:])
@@ -130,8 +128,8 @@ def tile_picked_slotadd_tanh_po_kernel(
             )
 
         quarters = [slice(0, S // 4), slice(S // 4, S // 2)]
-        parts = [(t, [cols]) for cols in quarters for t in (1, 0)]
-        parts = parts + [(0, [halves[1]]), (1, [halves[1]]), (2, [whole]), (LAST, [whole])]
+        parts = [(0, [quarters[0]]), (1, [quarters[0]]), (0, [quarters[1]]), (1, [quarters[1], halves[1]])]
+        parts = parts + [(0, [halves[1]]), (2, [whole]), (LAST, [whole])]
         products = {}
         for t, passes in parts:
             features = slice(t * P, (t + 1) * P)
@@ -152,45 +150,42 @@ def tile_picked_slotadd_tanh_po_kernel(
         def squash(t, first, out):
             nc.scalar.activation(out, products[t, first][:], TANH)
 
-        def scatter(t, h, update):
-            nc.vector.tensor_copy(memory[t][:].indirect(slot_list[:, list_halves[h]]), update[:])
-
-        early, y = values("y1_0", S // 2), values("y0_0", S // 2)
-        update = values("update1_0", S // 2)
-        for cols in quarters:
-            squash(1, cols.start, early[:, cols])
-            nc.vector.tensor_tensor(update[:, cols], early[:, cols], means[1][:, cols], ADD)
-            squash(0, cols.start, y[:, cols])
-        nc.vector.tensor_tensor(memory[0][:].indirect(slot_list[:, list_halves[0]]), y[:], first_mean[:], ADD)
-        scatter(1, 0, update)
-        for t in range(2):
-            y = values("y%d_1" % t, S // 2)
-            squash(t, S // 2, y[:])
-            if t == 0:
-                update = values("update0_1", S // 2, "y0_0")
-            else:
-                update = shared.tile([P, S // 2], F32, name="update1_1", offset=10752, align_bytes=64)
-            nc.gpsimd.tensor_tensor(update[:], y[:], means[t][:, halves[1]], ADD)
-            scatter(t, 1, update)
-            nc.sync.dma_start(out=out_rows[:, t, :], in_=memory[t][:])
+        ready = []
+        for n, (t, passes) in enumerate(parts[:5]):
+            first, last = passes[0].start, passes[-1].stop
+            y, update = values("y%d_%d" % (t, first), last - first), values("update%d_%d" % (t, first), last - first)
+            squash(t, first, y[:])
+            adder = nc.vector if first == 0 else nc.gpsimd
+            adder.tensor_tensor(update[:], y[:], means[t][:, first:last], ADD)
+            ready.append((t, first, last, update))
+            if n == 0:
+                continue
+            for plane, a, b, made in ready:
+                nc.vector.tensor_copy(memory[plane][:].indirect(slot_list[:, a // LIST_ROWS : b // LIST_ROWS]), made[:])
+            ready.clear()
+            if last == S:
+                nc.sync.dma_start(out=out_rows[:, t, :], in_=memory[t][:])
         at_from[2] = shared.tile([P, 3 * S], F32, name="from2", offset=2048, align_bytes=64)
         for t in range(2, PACK):
-            y = values("y%d" % t, S)
+            y = values("y%d" % t, S, "late_y")
             squash(t, 0, y[:])
             look_up(at_slot[t][:], t, slot_list)
-            partial = shared.tile([P, S], F32, name="partial%d" % t, offset=11776, align_bytes=64)
+            partial = values("partial%d" % t, S, "partial")
             nc.gpsimd.tensor_tensor(partial[:], y[:], at_slot[t][:], ADD)
             look_up(at_from[t][:, :S], t, from_list)
-            update = values("update%d" % t, S)
-            nc.gpsimd.tensor_tensor(update[:], partial[:], at_from[t][:, :S], ADD)
-            nc.vector.tensor_copy(memory[t][:].indirect(slot_list[:]), update[:])
+            if t == LAST:
+                nc.vector.tensor_tensor(memory[t][:].indirect(slot_list[:]), partial[:], at_from[t][:], ADD)
+            else:
+                update = values("update%d" % t, S)
+                nc.gpsimd.tensor_tensor(update[:], partial[:], at_from[t][:, :S], ADD)
+                nc.vector.tensor_copy(memory[t][:].indirect(slot_list[:]), update[:])
             nc.sync.dma_start(out=out_rows[:, t, :], in_=memory[t][:])
 
         places = (3072, 4096, 1024, 5120)
         pairs = [
             shared.tile([P, 2, b - a, 2], BF16, name="pairs%d" % a, offset=at, align_bytes=64) for (a, b), at in zip(PIECES, places)
         ]
-        pairs.append(keep.tile([P, 2, U - PIECES[-1][0], 2], BF16, name="last_pairs", tag="at_from3", align_bytes=64))
+        pairs.append(keep.tile([P, 2, U - PIECES[-1][0], 2], BF16, name="last_pairs", tag="at_slot3", align_bytes=64))
         rounded = [keep.tile([P, (b - a) * PACK], BF16, name="rounded%d" % a, align_bytes=64) for a, b in PIECES]
         out_codes = [keep.tile([P, b - a], I32, name="out_codes%d" % a, align_bytes=64) for a, b in STORES]
         out_scale = keep.tile([P, U], U8, name="out_scale", align_bytes=64)

@@ -128,8 +128,8 @@ def tile_picked_slotadd_tanh_po_kernel(
             )
 
         quarters = [slice(0, S // 4), slice(S // 4, S // 2)]
-        parts = [(0, [quarters[0]]), (1, [quarters[0]]), (0, [quarters[1]]), (1, [quarters[1], halves[1]])]
-        parts = parts + [(0, [halves[1]]), (2, [whole]), (LAST, [whole])]
+        parts = [(0, [quarters[0]]), (1, [quarters[0]]), (1, [quarters[1]]), (0, [quarters[1], halves[1]])]
+        parts = parts + [(1, [halves[1]]), (2, [whole]), (LAST, [whole])]
         products = {}
         for t, passes in parts:
             features = slice(t * P, (t + 1) * P)
@@ -150,21 +150,31 @@ def tile_picked_slotadd_tanh_po_kernel(
         def squash(t, first, out):
             nc.scalar.activation(out, products[t, first][:], TANH)
 
-        ready = []
-        for n, (t, passes) in enumerate(parts[:5]):
+        updates = [values("update%d" % t, S) for t in range(2)]
+
+        def finish(n):
+            t, passes = parts[n]
             first, last = passes[0].start, passes[-1].stop
-            y, update = values("y%d_%d" % (t, first), last - first), values("update%d_%d" % (t, first), last - first)
+            y = values("y%d_%d" % (t, first), last - first)
             squash(t, first, y[:])
             adder = nc.vector if first == 0 else nc.gpsimd
-            adder.tensor_tensor(update[:], y[:], means[t][:, first:last], ADD)
-            ready.append((t, first, last, update))
-            if n == 0:
-                continue
-            for plane, a, b, made in ready:
-                nc.vector.tensor_copy(memory[plane][:].indirect(slot_list[:, a // LIST_ROWS : b // LIST_ROWS]), made[:])
-            ready.clear()
+            adder.tensor_tensor(updates[t][:, first:last], y[:], means[t][:, first:last], ADD)
+
+        def scatter(t, first, last):
+            places = slot_list[:, first // LIST_ROWS : last // LIST_ROWS]
+            nc.vector.tensor_copy(memory[t][:].indirect(places), updates[t][:, first:last])
             if last == S:
                 nc.sync.dma_start(out=out_rows[:, t, :], in_=memory[t][:])
+
+        finish(0)
+        finish(1)
+        scatter(0, 0, S // 4)
+        finish(2)
+        scatter(1, 0, S // 2)
+        finish(3)
+        scatter(0, S // 4, S)
+        finish(4)
+        scatter(1, S // 2, S)
         at_from[2] = shared.tile([P, 3 * S], F32, name="from2", offset=2048, align_bytes=64)
         for t in range(2, PACK):
             y = values("y%d" % t, S, "late_y")

@@ -23,10 +23,13 @@ LAST = PACK - 1
 LIST_ROWS = 16
 SCALE_ROWS = K // 32
 QUADRANTS = 4
+FIRST, SECOND, REST, WHOLE = slice(0, S // 4), slice(S // 4, S // 2), slice(S // 2, S), slice(0, S)
+TURN = 3 * S // 8
+W_VECTOR = 112
 PIECES = ((0, 128), (128, 256), (256, 512), (512, 768), (768, U))
 STORES = ((0, 256), (256, 512), (512, 768), (768, U))
-SCALAR_WEAVES = 1
-W_VECTOR = 112
+FROM_AT, FROM_COLUMNS = 2048, 3 * S
+PAIRS_AT = (3072, 4096, 1024, 5120)
 
 
 def tile_picked_slotadd_tanh_po_kernel(
@@ -42,15 +45,20 @@ def tile_picked_slotadd_tanh_po_kernel(
         out_rows = out_0.rearrange("(p t) c -> p t c", t=PACK)
         w_rows = w1.rearrange("(p j) c -> p j c", j=PACK)
 
+        def values(name, width, tag=None):
+            return keep.tile([P, width], F32, name=name, tag=tag or name, align_bytes=64)
+
+        def entries(places, cols):
+            return places[:, cols.start // LIST_ROWS : cols.stop // LIST_ROWS]
+
         slot_list = keep.tile([P, S // LIST_ROWS], U16, name="slot_list")
         from_list = keep.tile([P, S // LIST_ROWS], U16, name="from_list")
         token_list = keep.tile([P, S // LIST_ROWS], U16, name="token_list")
-        memory = [keep.tile([P, U], F32, name="memory%d" % t, align_bytes=64) for t in range(2)]
+        planes = [values("plane%d" % t, U) for t in range(2)]
         w_raw = [keep.tile([P, PACK // 2, N], F32, name="w_raw%d" % h, align_bytes=64) for h in range(2)]
-        x_table = keep.tile([P, T], I32, name="x_table", align_bytes=64)
-        x_scale_table = keep.tile([P, T], U8, name="x_scale_table", align_bytes=64)
 
         scale_base = P - SCALE_ROWS
+        x_scale_table = keep.tile([P, T], U8, name="x_scale_table", align_bytes=64)
         x_scale_picked = keep.tile([P, S], U8, name="x_scale_picked", align_bytes=64)
         x_scale = keep.tile([P, S], U8, name="x_scale", align_bytes=64)
         nc.scalar.dma_start(out=x_scale_table[scale_base:, :].bitcast(I32), in_=x_scales[0].bitcast(I32))
@@ -61,57 +69,47 @@ def tile_picked_slotadd_tanh_po_kernel(
         nc.vector.memset(x_scale[:].bitcast(I32), 0)
 
         nc.sync.dma_start(token_list[:], offs)
-        nc.sync.dma_start(out=memory[0][:], in_=mem_rows[:, 0, :])
+        nc.sync.dma_start(out=planes[0][:], in_=mem_rows[:, 0, :])
         nc.sync.dma_start(slot_list[:], slot)
         nc.sync.dma_start(from_list[:], from_l)
         nc.sync.dma_start(out=w_raw[0][:], in_=w_rows[:, 0:2, :])
         nc.sync.dma_start(out=w_raw[1][:], in_=w_rows[:, 2:4, :])
-        nc.sync.dma_start(out=memory[1][:], in_=mem_rows[:, 1, :])
+        nc.sync.dma_start(out=planes[1][:], in_=mem_rows[:, 1, :])
+        x_table = keep.tile([P, T], I32, name="x_table", align_bytes=64)
         nc.sync.dma_start(out=x_table[:], in_=x_words[0].rearrange("p c r -> p (c r)").bitcast(I32))
 
-        halves = [slice(h * S // 2, (h + 1) * S // 2) for h in range(2)]
-        list_halves = [slice(h * S // LIST_ROWS // 2, (h + 1) * S // LIST_ROWS // 2) for h in range(2)]
-
-        at_slot = [keep.tile([P, S], F32, name="at_slot%d" % t, align_bytes=64) for t in range(PACK)]
-        at_from = [keep.tile([P, S], F32, name="at_from%d" % t, align_bytes=64) for t in range(PACK)]
-        means = [keep.tile([P, S], F32, name="mean%d" % t, align_bytes=64) for t in range(2)]
-        whole = slice(0, S)
-
-        def values(name, width, tag=None):
-            return keep.tile([P, width], F32, name=name, tag=tag or name, align_bytes=64)
-
         def look_up(out, t, places):
-            nc.scalar.activation(out, memory[t][:].indirect(places[:]), COPY, scale=0.5)
+            nc.scalar.activation(out, planes[t][:].indirect(places[:]), COPY, scale=0.5)
+
+        def look_up_both(t):
+            at_slot, at_from = values("at_slot%d" % t, S), values("at_from%d" % t, S)
+            nc.vector.tensor_scalar(at_slot[:], planes[t][:].indirect(slot_list[:]), 0.5, 0.0, MULT, ADD)
+            look_up(at_from[:], t, from_list)
+            return at_slot, at_from
 
         nc.vector.tensor_copy(x_scale_picked[:], x_scale_table[:].indirect(token_list[:]))
-        nc.vector.tensor_scalar(at_slot[0][:], memory[0][:].indirect(slot_list[:]), 0.5, 0.0, MULT, ADD)
-        nc.scalar.activation(at_from[0][:], memory[0][:].indirect(from_list[:]), COPY, scale=0.5)
-
-        def move_scales(q, cols):
-            nc.sync.dma_start(
-                out=x_scale[32 * q : 32 * q + 4, cols].bitcast(I32),
-                in_=x_scale_picked[scale_base + 4 * q : scale_base + 4 * q + 4, cols].bitcast(I32),
-            )
+        at_slot, at_from = look_up_both(0)
 
         for q in range(QUADRANTS):
-            move_scales(q, whole)
+            nc.sync.dma_start(
+                out=x_scale[32 * q : 32 * q + 4, :].bitcast(I32),
+                in_=x_scale_picked[scale_base + 4 * q : scale_base + 4 * q + 4, :].bitcast(I32),
+            )
 
         w_grouped = keep.tile([P, N * PACK], BF16, name="w_grouped", align_bytes=64)
         w_dealt = w_grouped[:].rearrange("p (t m j) -> p m t j", t=PACK, j=PACK)
         w_read = [half[:].rearrange("p j (m t) -> p m t j", t=PACK) for half in w_raw]
-        nc.vector.tensor_tensor(means[0][:], at_slot[0][:], at_from[0][:], ADD)
+        means = [values("mean%d" % t, S) for t in range(2)]
+        nc.vector.tensor_tensor(means[0][:], at_slot[:], at_from[:], ADD)
         nc.scalar.copy(w_dealt[:, :, :, 0:2], w_read[0])
         nc.vector.tensor_copy(w_dealt[:, :W_VECTOR, :, 2:4], w_read[1][:, :W_VECTOR])
         nc.scalar.copy(w_dealt[:, W_VECTOR:, :, 2:4], w_read[1][:, W_VECTOR:])
         for t, tag in enumerate(("x_scale_table", "w_raw0"), 2):
-            memory.append(keep.tile([P, U], F32, name="memory%d" % t, tag=tag, align_bytes=64))
-            nc.sync.dma_start(out=memory[t][:], in_=mem_rows[:, t, :])
+            planes.append(values("plane%d" % t, U, tag))
+            nc.sync.dma_start(out=planes[t][:], in_=mem_rows[:, t, :])
 
         x_codes = keep.tile([P, S], U32, name="x_codes", align_bytes=64)
-        w_codes = [
-            keep.tile([P, N // 2], U32, name="w_codes0", align_bytes=64),
-            keep.tile([P, N // 2], U32, name="w_codes1", align_bytes=64),
-        ]
+        w_codes = [keep.tile([P, N // 2], U32, name="w_codes%d" % u, align_bytes=64) for u in range(2)]
         w_scale = keep.tile([P, N], U8, name="w_scale", align_bytes=64)
         for u in range(2):
             nc.vector.quantize_mx(
@@ -119,94 +117,90 @@ def tile_picked_slotadd_tanh_po_kernel(
                 scales=w_scale[:, u * N // 2 : (u + 1) * N // 2],
                 in_=w_grouped[:, u * N * PACK // 2 : (u + 1) * N * PACK // 2],
             )
-        nc.vector.tensor_scalar(at_slot[1][:], memory[1][:].indirect(slot_list[:]), 0.5, 0.0, MULT, ADD)
-        look_up(at_from[1][:], 1, from_list)
-        nc.gpsimd.tensor_tensor(means[1][:], at_slot[1][:], at_from[1][:], ADD)
-        for first, last in ((0, S // 4), (S // 4, S // 2), (S // 2, S)):
-            nc.vector.tensor_copy(
-                x_codes[:, first:last], x_table[:].bitcast(U32).indirect(token_list[:, first // LIST_ROWS : last // LIST_ROWS])
+        at_slot, at_from = look_up_both(1)
+        nc.gpsimd.tensor_tensor(means[1][:], at_slot[:], at_from[:], ADD)
+        for cols in (FIRST, SECOND, REST):
+            nc.vector.tensor_copy(x_codes[:, cols], x_table[:].bitcast(U32).indirect(entries(token_list, cols)))
+
+        def multiply(t, cols, bank=None):
+            name = "product%d_%d" % (t, cols.start)
+            product = psum.tile([P, cols.stop - cols.start], F32, name=name, tag=bank or name)
+            nc.tensor.matmul_mx(
+                out=product[:],
+                lhsT=w_codes[t // 2][:, t % 2 * P : (t % 2 + 1) * P].bitcast(FP8X4),
+                lhsT_scale=w_scale[:, t * P : (t + 1) * P],
+                rhs=x_codes[:, cols].bitcast(FP8X4),
+                rhs_scale=x_scale[:, cols],
+                start=True,
+                stop=True,
             )
+            return product
 
-        quarters = [slice(0, S // 4), slice(S // 4, S // 2)]
-        parts = [(0, [quarters[0]]), (1, [quarters[0]]), (1, [quarters[1]]), (0, [quarters[1], halves[1]])]
-        parts = parts + [(1, [halves[1]]), (2, [whole]), (LAST, [whole])]
-        products = {}
-        for t, passes in parts:
-            features = slice(t * P, (t + 1) * P)
-            first = passes[0].start
-            product = psum.tile([P, passes[-1].stop - first], F32, name="product%d_%d" % (t, first))
-            for cols in passes:
-                nc.tensor.matmul_mx(
-                    out=product[:, cols.start - first : cols.stop - first],
-                    lhsT=w_codes[t // 2][:, t % 2 * P : (t % 2 + 1) * P].bitcast(FP8X4),
-                    lhsT_scale=w_scale[:, features],
-                    rhs=x_codes[:, cols].bitcast(FP8X4),
-                    rhs_scale=x_scale[:, cols],
-                    start=True,
-                    stop=True,
-                )
-            products[t, first] = product
+        def squash(t, cols, tag=None):
+            y = values("y%d_%d" % (t, cols.start), cols.stop - cols.start, tag)
+            nc.scalar.activation(y[:], multiply(t, cols)[:], TANH)
+            return y
 
-        def squash(t, first, out):
-            nc.scalar.activation(out, products[t, first][:], TANH)
+        updates = [values("update%d" % t, S) for t in range(LAST)]
 
-        updates = [values("update%d" % t, S) for t in range(2)]
+        def add_mean(t, cols, adder):
+            adder.tensor_tensor(updates[t][:, cols], squash(t, cols)[:], means[t][:, cols], ADD)
 
-        def finish(n):
-            t, passes = parts[n]
-            first, last = passes[0].start, passes[-1].stop
-            y = values("y%d_%d" % (t, first), last - first)
-            squash(t, first, y[:])
-            adder = nc.vector if first == 0 else nc.gpsimd
-            adder.tensor_tensor(updates[t][:, first:last], y[:], means[t][:, first:last], ADD)
+        def scatter(t, cols):
+            nc.vector.tensor_copy(planes[t][:].indirect(entries(slot_list, cols)), updates[t][:, cols])
+            if cols.stop == S:
+                nc.sync.dma_start(out=out_rows[:, t, :], in_=planes[t][:])
 
-        def scatter(t, first, last):
-            places = slot_list[:, first // LIST_ROWS : last // LIST_ROWS]
-            nc.vector.tensor_copy(memory[t][:].indirect(places), updates[t][:, first:last])
-            if last == S:
-                nc.sync.dma_start(out=out_rows[:, t, :], in_=memory[t][:])
+        add_mean(0, FIRST, nc.vector)
+        add_mean(1, FIRST, nc.vector)
+        scatter(0, FIRST)
+        add_mean(1, slice(FIRST.stop, TURN), nc.gpsimd)
+        scatter(1, slice(0, TURN))
+        add_mean(0, SECOND, nc.gpsimd)
+        add_mean(0, REST, nc.gpsimd)
+        scatter(0, slice(FIRST.stop, S))
+        y = values("y1_last", S - TURN)
+        nc.scalar.activation(y[:, : REST.start - TURN], multiply(1, slice(TURN, REST.start), "product0_0")[:], TANH)
+        nc.scalar.activation(y[:, REST.start - TURN :], multiply(1, REST)[:], TANH)
+        nc.gpsimd.tensor_tensor(updates[1][:, TURN:], y[:], means[1][:, TURN:], ADD)
+        scatter(1, slice(TURN, S))
 
-        finish(0)
-        finish(1)
-        scatter(0, 0, S // 4)
-        finish(2)
-        scatter(1, 0, S // 2)
-        finish(3)
-        scatter(0, S // 4, S)
-        finish(4)
-        scatter(1, S // 2, S)
-        at_from[2] = shared.tile([P, 3 * S], F32, name="from2", offset=2048, align_bytes=64)
-        for t in range(2, PACK):
-            y = values("y%d" % t, S, "late_y")
-            squash(t, 0, y[:])
-            look_up(at_slot[t][:], t, slot_list)
-            partial = values("partial%d" % t, S, "partial")
-            nc.gpsimd.tensor_tensor(partial[:], y[:], at_slot[t][:], ADD)
-            look_up(at_from[t][:, :S], t, from_list)
-            if t == LAST:
-                nc.vector.tensor_tensor(memory[t][:].indirect(slot_list[:]), partial[:], at_from[t][:], ADD)
-            else:
-                update = values("update%d" % t, S)
-                nc.gpsimd.tensor_tensor(update[:], partial[:], at_from[t][:, :S], ADD)
-                nc.vector.tensor_copy(memory[t][:].indirect(slot_list[:]), update[:])
-            nc.sync.dma_start(out=out_rows[:, t, :], in_=memory[t][:])
+        y = squash(2, WHOLE, "late_y")
+        at_slot = values("at_slot2", S)
+        look_up(at_slot[:], 2, slot_list)
+        partial = values("partial2", S, "partial")
+        nc.gpsimd.tensor_tensor(partial[:], y[:], at_slot[:], ADD)
+        at_from = shared.tile([P, FROM_COLUMNS], F32, name="at_from2", offset=FROM_AT, align_bytes=64)
+        look_up(at_from[:, :S], 2, from_list)
+        nc.gpsimd.tensor_tensor(updates[2][:], partial[:], at_from[:, :S], ADD)
+        scatter(2, WHOLE)
 
-        places = (3072, 4096, 1024, 5120)
+        y = squash(LAST, WHOLE, "late_y")
+        at_slot = values("at_slot3", S)
+        look_up(at_slot[:], LAST, slot_list)
+        partial = values("partial3", S, "partial")
+        nc.gpsimd.tensor_tensor(partial[:], y[:], at_slot[:], ADD)
+        at_from = values("at_from3", S)
+        look_up(at_from[:], LAST, from_list)
+        nc.vector.tensor_tensor(planes[LAST][:].indirect(slot_list[:]), partial[:], at_from[:], ADD)
+        nc.sync.dma_start(out=out_rows[:, LAST, :], in_=planes[LAST][:])
+
         pairs = [
-            shared.tile([P, 2, b - a, 2], BF16, name="pairs%d" % a, offset=at, align_bytes=64) for (a, b), at in zip(PIECES, places)
+            shared.tile([P, 2, b - a, 2], BF16, name="pairs%d" % a, offset=at, align_bytes=64)
+            for (a, b), at in zip(PIECES, PAIRS_AT)
         ]
-        pairs.append(keep.tile([P, 2, U - PIECES[-1][0], 2], BF16, name="last_pairs", tag="at_slot3", align_bytes=64))
+        final = len(PIECES) - 1
+        pairs.append(keep.tile([P, 2, U - PIECES[final][0], 2], BF16, name="last_pairs", tag="at_slot3", align_bytes=64))
         rounded = [keep.tile([P, (b - a) * PACK], BF16, name="rounded%d" % a, align_bytes=64) for a, b in PIECES]
         out_codes = [keep.tile([P, b - a], I32, name="out_codes%d" % a, align_bytes=64) for a, b in STORES]
         out_scale = keep.tile([P, U], U8, name="out_scale", align_bytes=64)
         out_words = out_1[0].rearrange("p c r -> p (c r)").bitcast(I32)
-        by_vector = len(PIECES) - SCALAR_WEAVES
         for t in range(PACK):
             for n, (a, b) in enumerate(PIECES):
-                copy = nc.vector.tensor_copy if t >= 2 and n >= by_vector else nc.scalar.copy
-                copy(pairs[n][:, t // 2, :, t % 2], memory[t][:, a:b])
+                copy = nc.vector.tensor_copy if t >= 2 and n == final else nc.scalar.copy
+                copy(pairs[n][:, t // 2, :, t % 2], planes[t][:, a:b])
 
-        def weave(n, copy, dtype):
+        def regroup(n, copy, dtype):
             words = pairs[n][:].rearrange("p u c e -> p (u c e)").bitcast(dtype).rearrange("p (u c) -> p c u", u=2)
             copy(rounded[n][:].bitcast(dtype).rearrange("p (c u) -> p c u", u=2), words)
 
@@ -220,14 +214,13 @@ def tile_picked_slotadd_tanh_po_kernel(
             if last == b:
                 nc.sync.dma_start(out=out_words[:, a:b], in_=out_codes[m][:])
 
-        for n in range(by_vector, len(PIECES)):
-            weave(n, nc.scalar.copy, U32)
-        for n in range(by_vector):
-            weave(n, nc.vector.tensor_copy, I32)
+        regroup(final, nc.scalar.copy, U32)
+        for n in range(final):
+            regroup(n, nc.vector.tensor_copy, I32)
             if n > 0:
                 quantise(n - 1)
-        for n in range(by_vector - 1, len(PIECES)):
-            quantise(n)
+        quantise(final - 1)
+        quantise(final)
         for q in range(QUADRANTS):
             queue = nc.scalar if q % 2 == 0 else nc.sync
             queue.dma_start(

@@ -26,10 +26,10 @@ QUADRANTS = 4
 FIRST, SECOND, REST, WHOLE = slice(0, S // 4), slice(S // 4, S // 2), slice(S // 2, S), slice(0, S)
 TURN = 3 * S // 8
 W_VECTOR = 112
-PIECES = ((0, 128), (128, 256), (256, 512), (512, 768), (768, U))
-STORES = ((0, 256), (256, 512), (512, 768), (768, U))
-FROM_AT, FROM_COLUMNS = 2048, 3 * S
-PAIRS_AT = (3072, 4096, 1024, 5120)
+PIECES = ((0, 256), (256, 512), (512, 768), (768, U))
+STORES = ((0, 512), (512, 768), (768, U))
+FROM_AT, FROM_COLUMNS = 1024, 3 * S
+PAIRS_AT = (0, 2048, 4096, 6144)
 
 
 def tile_picked_slotadd_tanh_po_kernel(
@@ -190,15 +190,10 @@ def tile_picked_slotadd_tanh_po_kernel(
             for (a, b), at in zip(PIECES, PAIRS_AT)
         ]
         final = len(PIECES) - 1
-        pairs.append(keep.tile([P, 2, U - PIECES[final][0], 2], BF16, name="last_pairs", tag="at_slot3", align_bytes=64))
         rounded = [keep.tile([P, (b - a) * PACK], BF16, name="rounded%d" % a, align_bytes=64) for a, b in PIECES]
         out_codes = [keep.tile([P, b - a], I32, name="out_codes%d" % a, align_bytes=64) for a, b in STORES]
         out_scale = keep.tile([P, U], U8, name="out_scale", align_bytes=64)
         out_words = out_1[0].rearrange("p c r -> p (c r)").bitcast(I32)
-        for t in range(PACK):
-            for n, (a, b) in enumerate(PIECES):
-                copy = nc.vector.tensor_copy if t >= 2 and n == final else nc.scalar.copy
-                copy(pairs[n][:, t // 2, :, t % 2], planes[t][:, a:b])
 
         def regroup(n, copy, dtype):
             words = pairs[n][:].rearrange("p u c e -> p (u c e)").bitcast(dtype).rearrange("p (u c) -> p c u", u=2)
@@ -214,11 +209,21 @@ def tile_picked_slotadd_tanh_po_kernel(
             if last == b:
                 nc.sync.dma_start(out=out_words[:, a:b], in_=out_codes[m][:])
 
+        for t in range(2):
+            for n, (a, b) in enumerate(PIECES):
+                nc.scalar.copy(pairs[n][:, 0, :, t], planes[t][:, a:b])
+        a, b = PIECES[0]
+        nc.scalar.copy(pairs[0][:, 1], planes[2][:, a:b].unsqueeze(2).to_broadcast([P, b - a, 2]))
+        regroup(0, nc.scalar.copy, U32)
+        for t in range(2, PACK):
+            for n, (a, b) in list(enumerate(PIECES))[1:]:
+                nc.scalar.copy(pairs[n][:, 1, :, t % 2], planes[t][:, a:b])
+        a, b = PIECES[0]
+        nc.vector.tensor_copy(rounded[0][:].rearrange("p (c t) -> p c t", t=PACK)[:, :, LAST], planes[LAST][:, a:b])
         regroup(final, nc.scalar.copy, U32)
-        for n in range(final):
+        for n in range(1, final):
             regroup(n, nc.vector.tensor_copy, I32)
-            if n > 0:
-                quantise(n - 1)
+            quantise(n - 1)
         quantise(final - 1)
         quantise(final)
         for q in range(QUADRANTS):

@@ -27,6 +27,7 @@ FIRST, SECOND, REST, WHOLE = slice(0, S // 4), slice(S // 4, S // 2), slice(S //
 TURN = 3 * S // 8
 W_VECTOR = 112
 PIECES = ((0, 256), (256, 512), (512, 768), (768, U))
+GPSIMD_FROM = 2
 STORES = ((0, 512), (512, 768), (768, U))
 FROM_AT, FROM_COLUMNS = 1024, 3 * S
 PAIRS_AT = (0, 2048, 4096, 6144)
@@ -141,7 +142,7 @@ def tile_picked_slotadd_tanh_po_kernel(
             nc.scalar.activation(y[:], multiply(t, cols)[:], TANH)
             return y
 
-        updates = [values("update%d" % t, S) for t in range(LAST)]
+        updates = [values("update%d" % t, S) for t in range(PACK)]
 
         def add_mean(t, cols, adder):
             adder.tensor_tensor(updates[t][:, cols], squash(t, cols)[:], means[t][:, cols], ADD)
@@ -182,8 +183,8 @@ def tile_picked_slotadd_tanh_po_kernel(
         nc.gpsimd.tensor_tensor(partial[:], y[:], at_slot[:], ADD)
         at_from = values("at_from3", S)
         look_up(at_from[:], LAST, from_list)
-        nc.vector.tensor_tensor(planes[LAST][:].indirect(slot_list[:]), partial[:], at_from[:], ADD)
-        nc.sync.dma_start(out=out_rows[:, LAST, :], in_=planes[LAST][:])
+        nc.gpsimd.tensor_tensor(updates[LAST][:], partial[:], at_from[:], ADD)
+        scatter(LAST, WHOLE)
 
         pairs = [
             shared.tile([P, 2, b - a, 2], BF16, name="pairs%d" % a, offset=at, align_bytes=64)
@@ -211,7 +212,10 @@ def tile_picked_slotadd_tanh_po_kernel(
 
         for t in range(2):
             for n, (a, b) in enumerate(PIECES):
-                nc.scalar.copy(pairs[n][:, 0, :, t], planes[t][:, a:b])
+                if n >= GPSIMD_FROM:
+                    nc.gpsimd.tensor_scalar(pairs[n][:, 0, :, t], planes[t][:, a:b], 1.0, 0.0, MULT, ADD)
+                else:
+                    nc.scalar.copy(pairs[n][:, 0, :, t], planes[t][:, a:b])
         a, b = PIECES[0]
         nc.scalar.copy(pairs[0][:, 1], planes[2][:, a:b].unsqueeze(2).to_broadcast([P, b - a, 2]))
         regroup(0, nc.scalar.copy, U32)

@@ -27,10 +27,11 @@ FIRST, SECOND, REST, WHOLE = slice(0, S // 4), slice(S // 4, S // 2), slice(S //
 TURN = 3 * S // 8
 W_VECTOR = 112
 PIECES = ((0, 256), (256, 512), (512, 768), (768, U))
-GPSIMD_FROM = 2
 STORES = ((0, 512), (512, 768), (768, U))
-FROM_AT, FROM_COLUMNS = 1024, 3 * S
-PAIRS_AT = (0, 2048, 4096, 6144)
+EARLY = ((0, 256), (512, 576), (256, 512))
+LATE = ((576, 768), (768, U))
+FROM_AT = (1024, 5632)
+PAIRS_AT = (0, 2048, 2560, 4608, 6144)
 
 
 def tile_picked_slotadd_tanh_po_kernel(
@@ -171,9 +172,9 @@ def tile_picked_slotadd_tanh_po_kernel(
         look_up(at_slot[:], 2, slot_list)
         partial = values("partial2", S, "partial")
         nc.gpsimd.tensor_tensor(partial[:], y[:], at_slot[:], ADD)
-        at_from = shared.tile([P, FROM_COLUMNS], F32, name="at_from2", offset=FROM_AT, align_bytes=64)
-        look_up(at_from[:, :S], 2, from_list)
-        nc.gpsimd.tensor_tensor(updates[2][:], partial[:], at_from[:, :S], ADD)
+        at_from = shared.tile([P, S], F32, name="at_from2", offset=FROM_AT[0], align_bytes=64)
+        look_up(at_from[:], 2, from_list)
+        nc.gpsimd.tensor_tensor(updates[2][:], partial[:], at_from[:], ADD)
         scatter(2, WHOLE)
 
         y = squash(LAST, WHOLE, "late_y")
@@ -181,24 +182,29 @@ def tile_picked_slotadd_tanh_po_kernel(
         look_up(at_slot[:], LAST, slot_list)
         partial = values("partial3", S, "partial")
         nc.gpsimd.tensor_tensor(partial[:], y[:], at_slot[:], ADD)
-        at_from = values("at_from3", S)
+        at_from = shared.tile([P, S], F32, name="at_from3", offset=FROM_AT[1], align_bytes=64)
         look_up(at_from[:], LAST, from_list)
         nc.gpsimd.tensor_tensor(updates[LAST][:], partial[:], at_from[:], ADD)
         scatter(LAST, WHOLE)
 
-        pairs = [
-            shared.tile([P, 2, b - a, 2], BF16, name="pairs%d" % a, offset=at, align_bytes=64)
-            for (a, b), at in zip(PIECES, PAIRS_AT)
-        ]
-        final = len(PIECES) - 1
+        pairs = {
+            a: shared.tile([P, 2, b - a, 2], BF16, name="pairs%d" % a, offset=at, align_bytes=64)
+            for (a, b), at in zip(EARLY + LATE, PAIRS_AT)
+        }
         rounded = [keep.tile([P, (b - a) * PACK], BF16, name="rounded%d" % a, align_bytes=64) for a, b in PIECES]
-        out_codes = [keep.tile([P, b - a], I32, name="out_codes%d" % a, align_bytes=64) for a, b in STORES]
+        a, b = STORES[0]
+        out_codes = [shared.tile([P, b - a], I32, name="out_codes0", offset=PAIRS_AT[len(EARLY) - 1], align_bytes=64)]
+        out_codes.extend(keep.tile([P, b - a], I32, name="out_codes%d" % a, align_bytes=64) for a, b in STORES[1:])
         out_scale = keep.tile([P, U], U8, name="out_scale", align_bytes=64)
         out_words = out_1[0].rearrange("p c r -> p (c r)").bitcast(I32)
 
-        def regroup(n, copy, dtype):
-            words = pairs[n][:].rearrange("p u c e -> p (u c e)").bitcast(dtype).rearrange("p (u c) -> p c u", u=2)
-            copy(rounded[n][:].bitcast(dtype).rearrange("p (c u) -> p c u", u=2), words)
+        def rounded_columns(a, b):
+            n = [first <= a and b <= last for first, last in PIECES].index(True)
+            return rounded[n][:, (a - PIECES[n][0]) * PACK : (b - PIECES[n][0]) * PACK]
+
+        def regroup(a, b):
+            words = pairs[a][:].rearrange("p u c e -> p (u c e)").bitcast(U32).rearrange("p (u c) -> p c u", u=2)
+            nc.scalar.copy(rounded_columns(a, b).bitcast(U32).rearrange("p (c u) -> p c u", u=2), words)
 
         def quantise(n):
             first, last = PIECES[n]
@@ -210,26 +216,29 @@ def tile_picked_slotadd_tanh_po_kernel(
             if last == b:
                 nc.sync.dma_start(out=out_words[:, a:b], in_=out_codes[m][:])
 
-        for t in range(2):
-            for n, (a, b) in enumerate(PIECES):
-                if n >= GPSIMD_FROM:
-                    nc.gpsimd.tensor_scalar(pairs[n][:, 0, :, t], planes[t][:, a:b], 1.0, 0.0, MULT, ADD)
-                else:
-                    nc.scalar.copy(pairs[n][:, 0, :, t], planes[t][:, a:b])
-        a, b = PIECES[0]
-        nc.scalar.copy(pairs[0][:, 1], planes[2][:, a:b].unsqueeze(2).to_broadcast([P, b - a, 2]))
-        regroup(0, nc.scalar.copy, U32)
-        for t in range(2, PACK):
-            for n, (a, b) in list(enumerate(PIECES))[1:]:
-                nc.scalar.copy(pairs[n][:, 1, :, t % 2], planes[t][:, a:b])
-        a, b = PIECES[0]
-        nc.vector.tensor_copy(rounded[0][:].rearrange("p (c t) -> p c t", t=PACK)[:, :, LAST], planes[LAST][:, a:b])
-        regroup(final, nc.scalar.copy, U32)
-        for n in range(1, final):
-            regroup(n, nc.vector.tensor_copy, I32)
-            quantise(n - 1)
-        quantise(final - 1)
-        quantise(final)
+        def twice(a, b):
+            return planes[2][:, a:b].unsqueeze(2).to_broadcast([P, b - a, 2])
+
+        for a, b in EARLY:
+            for t in range(2):
+                nc.scalar.copy(pairs[a][:, 0, :, t], planes[t][:, a:b])
+        for a, b in LATE:
+            for t in range(2):
+                nc.gpsimd.tensor_scalar(pairs[a][:, 0, :, t], planes[t][:, a:b], 1.0, 0.0, MULT, ADD)
+        for a, b in LATE:
+            nc.gpsimd.tensor_scalar(pairs[a][:, 1], twice(a, b), 1.0, 0.0, MULT, ADD)
+        for a, b in EARLY:
+            nc.scalar.copy(pairs[a][:, 1], twice(a, b))
+            regroup(a, b)
+        for a, b in EARLY:
+            nc.vector.tensor_copy(
+                rounded_columns(a, b).rearrange("p (c t) -> p c t", t=PACK)[:, :, LAST], planes[LAST][:, a:b]
+            )
+        for a, b in LATE:
+            nc.scalar.copy(pairs[a][:, 1, :, 1], planes[LAST][:, a:b])
+            regroup(a, b)
+        for n in range(len(PIECES)):
+            quantise(n)
         for q in range(QUADRANTS):
             queue = nc.scalar if q % 2 == 0 else nc.sync
             queue.dma_start(

@@ -25,13 +25,13 @@ SCALE_ROWS = K // 32
 QUADRANTS = 4
 FIRST, SECOND, REST, WHOLE = slice(0, S // 4), slice(S // 4, S // 2), slice(S // 2, S), slice(0, S)
 TURN = 3 * S // 8
-W_VECTOR = 112
-PIECES = ((0, 256), (256, 512), (512, 768), (768, U))
-STORES = ((0, 512), (512, 768), (768, U))
-EARLY = ((0, 256), (512, 576), (256, 512))
+W_VECTOR = 64
+PIECES = ((0, 384), (384, 768), (768, U))
+STORES = PIECES
+EARLY = ((0, 384), (384, 576))
 LATE = ((576, 768), (768, U))
-FROM_AT = (1024, 5632)
-PAIRS_AT = (0, 2048, 2560, 4608, 6144)
+FROM_AT = (2048, 5632)
+PAIRS_AT = (0, 3072, 4608, 6144)
 
 
 def tile_picked_slotadd_tanh_po_kernel(
@@ -57,7 +57,7 @@ def tile_picked_slotadd_tanh_po_kernel(
         from_list = keep.tile([P, S // LIST_ROWS], U16, name="from_list")
         token_list = keep.tile([P, S // LIST_ROWS], U16, name="token_list")
         planes = [values("plane%d" % t, U) for t in range(2)]
-        w_raw = [keep.tile([P, PACK // 2, N], F32, name="w_raw%d" % h, align_bytes=64) for h in range(2)]
+        w_raw = keep.tile([P, PACK, N], F32, name="w_raw", align_bytes=64)
 
         scale_base = P - SCALE_ROWS
         x_scale_table = keep.tile([P, T], U8, name="x_scale_table", align_bytes=64)
@@ -74,8 +74,7 @@ def tile_picked_slotadd_tanh_po_kernel(
         nc.sync.dma_start(out=planes[0][:], in_=mem_rows[:, 0, :])
         nc.sync.dma_start(slot_list[:], slot)
         nc.sync.dma_start(from_list[:], from_l)
-        nc.sync.dma_start(out=w_raw[0][:], in_=w_rows[:, 0:2, :])
-        nc.sync.dma_start(out=w_raw[1][:], in_=w_rows[:, 2:4, :])
+        nc.sync.dma_start(out=w_raw[:], in_=w_rows)
         nc.sync.dma_start(out=planes[1][:], in_=mem_rows[:, 1, :])
         x_table = keep.tile([P, T], I32, name="x_table", align_bytes=64)
         nc.sync.dma_start(out=x_table[:], in_=x_words[0].rearrange("p c r -> p (c r)").bitcast(I32))
@@ -100,13 +99,12 @@ def tile_picked_slotadd_tanh_po_kernel(
 
         w_grouped = keep.tile([P, N * PACK], BF16, name="w_grouped", align_bytes=64)
         w_dealt = w_grouped[:].rearrange("p (t m j) -> p m t j", t=PACK, j=PACK)
-        w_read = [half[:].rearrange("p j (m t) -> p m t j", t=PACK) for half in w_raw]
+        w_read = w_raw[:].rearrange("p j (m t) -> p m t j", t=PACK)
         means = [values("mean%d" % t, S) for t in range(2)]
         nc.vector.tensor_tensor(means[0][:], at_slot[:], at_from[:], ADD)
-        nc.scalar.copy(w_dealt[:, :, :, 0:2], w_read[0])
-        nc.vector.tensor_copy(w_dealt[:, :W_VECTOR, :, 2:4], w_read[1][:, :W_VECTOR])
-        nc.scalar.copy(w_dealt[:, W_VECTOR:, :, 2:4], w_read[1][:, W_VECTOR:])
-        for t, tag in enumerate(("x_scale_table", "w_raw0"), 2):
+        nc.vector.tensor_copy(w_dealt[:, :W_VECTOR], w_read[:, :W_VECTOR])
+        nc.scalar.copy(w_dealt[:, W_VECTOR:], w_read[:, W_VECTOR:])
+        for t, tag in enumerate(("x_scale_table", "w_raw"), 2):
             planes.append(values("plane%d" % t, U, tag))
             nc.sync.dma_start(out=planes[t][:], in_=mem_rows[:, t, :])
 

@@ -25,7 +25,7 @@ SCALE_ROWS = K // 32
 QUADRANTS = 4
 FIRST, SECOND, REST, WHOLE = slice(0, S // 4), slice(S // 4, S // 2), slice(S // 2, S), slice(0, S)
 TURN = 3 * S // 8
-W_VECTOR = 64
+W_VECTOR = 88
 PIECES = ((0, 384), (384, 768), (768, U))
 STORES = PIECES
 EARLY = ((0, 384), (384, 576))
@@ -79,17 +79,20 @@ def tile_picked_slotadd_tanh_po_kernel(
         x_table = keep.tile([P, T], I32, name="x_table", align_bytes=64)
         nc.sync.dma_start(out=x_table[:], in_=x_words[0].rearrange("p c r -> p (c r)").bitcast(I32))
 
-        def look_up(out, t, places):
-            nc.scalar.activation(out, planes[t][:].indirect(places[:]), COPY, scale=0.5)
+        def look_up(out, t, places, cols=WHOLE):
+            nc.scalar.activation(out, planes[t][:].indirect(entries(places, cols)), COPY, scale=0.5)
 
-        def look_up_both(t):
+        def look_up_both(t, on_vector):
             at_slot, at_from = values("at_slot%d" % t, S), values("at_from%d" % t, S)
-            nc.vector.tensor_scalar(at_slot[:], planes[t][:].indirect(slot_list[:]), 0.5, 0.0, MULT, ADD)
+            head = entries(slot_list, slice(0, on_vector))
+            nc.vector.tensor_scalar(at_slot[:, :on_vector], planes[t][:].indirect(head), 0.5, 0.0, MULT, ADD)
             look_up(at_from[:], t, from_list)
+            if on_vector < S:
+                look_up(at_slot[:, on_vector:], t, slot_list, slice(on_vector, S))
             return at_slot, at_from
 
         nc.vector.tensor_copy(x_scale_picked[:], x_scale_table[:].indirect(token_list[:]))
-        at_slot, at_from = look_up_both(0)
+        at_slot, at_from = look_up_both(0, S)
 
         for q in range(QUADRANTS):
             nc.sync.dma_start(
@@ -117,7 +120,7 @@ def tile_picked_slotadd_tanh_po_kernel(
                 scales=w_scale[:, u * N // 2 : (u + 1) * N // 2],
                 in_=w_grouped[:, u * N * PACK // 2 : (u + 1) * N * PACK // 2],
             )
-        at_slot, at_from = look_up_both(1)
+        at_slot, at_from = look_up_both(1, S // 2)
         nc.gpsimd.tensor_tensor(means[1][:], at_slot[:], at_from[:], ADD)
         for cols in (FIRST, SECOND, REST):
             nc.vector.tensor_copy(x_codes[:, cols], x_table[:].bitcast(U32).indirect(entries(token_list, cols)))

@@ -27,11 +27,10 @@ FIRST, SECOND, REST, WHOLE = slice(0, S // 4), slice(S // 4, S // 2), slice(S //
 TURN = 3 * S // 8
 W_VECTOR = 88
 PIECES = ((0, 384), (384, 768), (768, U))
-STORES = PIECES
 EARLY = ((0, 384), (384, 576))
 LATE = ((576, 768), (768, U))
-FROM_AT = (2048, 5632)
 PAIRS_AT = (0, 3072, 4608, 6144)
+FROM_AT = (2816, 6144)
 
 
 def tile_picked_slotadd_tanh_po_kernel(
@@ -70,10 +69,10 @@ def tile_picked_slotadd_tanh_po_kernel(
         nc.vector.memset(x_scale_table[:scale_base, :].bitcast(I32), 0)
         nc.vector.memset(x_scale[:].bitcast(I32), 0)
 
-        nc.sync.dma_start(token_list[:], offs)
         nc.sync.dma_start(out=planes[0][:], in_=mem_rows[:, 0, :])
         nc.sync.dma_start(slot_list[:], slot)
         nc.sync.dma_start(from_list[:], from_l)
+        nc.sync.dma_start(token_list[:], offs)
         nc.sync.dma_start(out=w_raw[:], in_=w_rows)
         nc.sync.dma_start(out=planes[1][:], in_=mem_rows[:, 1, :])
         x_table = keep.tile([P, T], I32, name="x_table", align_bytes=64)
@@ -82,17 +81,16 @@ def tile_picked_slotadd_tanh_po_kernel(
         def look_up(out, t, places, cols=WHOLE):
             nc.scalar.activation(out, planes[t][:].indirect(entries(places, cols)), COPY, scale=0.5)
 
-        def look_up_both(t, on_vector):
+        def look_up_both(t):
             at_slot, at_from = values("at_slot%d" % t, S), values("at_from%d" % t, S)
-            head = entries(slot_list, slice(0, on_vector))
-            nc.vector.tensor_scalar(at_slot[:, :on_vector], planes[t][:].indirect(head), 0.5, 0.0, MULT, ADD)
+            head = slice(0, REST.start)
+            nc.vector.tensor_scalar(at_slot[:, head], planes[t][:].indirect(entries(slot_list, head)), 0.5, 0.0, MULT, ADD)
             look_up(at_from[:], t, from_list)
-            if on_vector < S:
-                look_up(at_slot[:, on_vector:], t, slot_list, slice(on_vector, S))
+            look_up(at_slot[:, REST], t, slot_list, REST)
             return at_slot, at_from
 
+        at_slot, at_from = look_up_both(0)
         nc.vector.tensor_copy(x_scale_picked[:], x_scale_table[:].indirect(token_list[:]))
-        at_slot, at_from = look_up_both(0, S)
 
         for q in range(QUADRANTS):
             nc.sync.dma_start(
@@ -120,7 +118,7 @@ def tile_picked_slotadd_tanh_po_kernel(
                 scales=w_scale[:, u * N // 2 : (u + 1) * N // 2],
                 in_=w_grouped[:, u * N * PACK // 2 : (u + 1) * N * PACK // 2],
             )
-        at_slot, at_from = look_up_both(1, S // 2)
+        at_slot, at_from = look_up_both(1)
         nc.gpsimd.tensor_tensor(means[1][:], at_slot[:], at_from[:], ADD)
         for cols in (FIRST, SECOND, REST):
             nc.vector.tensor_copy(x_codes[:, cols], x_table[:].bitcast(U32).indirect(entries(token_list, cols)))
@@ -168,34 +166,25 @@ def tile_picked_slotadd_tanh_po_kernel(
         nc.gpsimd.tensor_tensor(updates[1][:, TURN:], y[:], means[1][:, TURN:], ADD)
         scatter(1, slice(TURN, S))
 
-        y = squash(2, WHOLE, "late_y")
-        at_slot = values("at_slot2", S)
-        look_up(at_slot[:], 2, slot_list)
-        partial = values("partial2", S, "partial")
-        nc.gpsimd.tensor_tensor(partial[:], y[:], at_slot[:], ADD)
-        at_from = shared.tile([P, S], F32, name="at_from2", offset=FROM_AT[0], align_bytes=64)
-        look_up(at_from[:], 2, from_list)
-        nc.gpsimd.tensor_tensor(updates[2][:], partial[:], at_from[:], ADD)
-        scatter(2, WHOLE)
-
-        y = squash(LAST, WHOLE, "late_y")
-        at_slot = values("at_slot3", S)
-        look_up(at_slot[:], LAST, slot_list)
-        partial = values("partial3", S, "partial")
-        nc.gpsimd.tensor_tensor(partial[:], y[:], at_slot[:], ADD)
-        at_from = shared.tile([P, S], F32, name="at_from3", offset=FROM_AT[1], align_bytes=64)
-        look_up(at_from[:], LAST, from_list)
-        nc.gpsimd.tensor_tensor(updates[LAST][:], partial[:], at_from[:], ADD)
-        scatter(LAST, WHOLE)
+        for t, at in enumerate(FROM_AT, 2):
+            y = squash(t, WHOLE, "late_y")
+            at_slot = values("at_slot%d" % t, S)
+            look_up(at_slot[:], t, slot_list)
+            partial = values("partial%d" % t, S, "partial")
+            nc.gpsimd.tensor_tensor(partial[:], y[:], at_slot[:], ADD)
+            at_from = shared.tile([P, S], F32, name="at_from%d" % t, offset=at, align_bytes=64)
+            look_up(at_from[:], t, from_list)
+            nc.gpsimd.tensor_tensor(updates[t][:], partial[:], at_from[:], ADD)
+            scatter(t, WHOLE)
 
         pairs = {
             a: shared.tile([P, 2, b - a, 2], BF16, name="pairs%d" % a, offset=at, align_bytes=64)
             for (a, b), at in zip(EARLY + LATE, PAIRS_AT)
         }
         rounded = [keep.tile([P, (b - a) * PACK], BF16, name="rounded%d" % a, align_bytes=64) for a, b in PIECES]
-        a, b = STORES[0]
-        out_codes = [shared.tile([P, b - a], I32, name="out_codes0", offset=PAIRS_AT[len(EARLY) - 1], align_bytes=64)]
-        out_codes.extend(keep.tile([P, b - a], I32, name="out_codes%d" % a, align_bytes=64) for a, b in STORES[1:])
+        a, b = PIECES[0]
+        out_codes = [shared.tile([P, b - a], I32, name="out_codes0", offset=PAIRS_AT[1], align_bytes=64)]
+        out_codes.extend(keep.tile([P, b - a], I32, name="out_codes%d" % a, align_bytes=64) for a, b in PIECES[1:])
         out_scale = keep.tile([P, U], U8, name="out_scale", align_bytes=64)
         out_words = out_1[0].rearrange("p c r -> p (c r)").bitcast(I32)
 
@@ -207,30 +196,25 @@ def tile_picked_slotadd_tanh_po_kernel(
             words = pairs[a][:].rearrange("p u c e -> p (u c e)").bitcast(U32).rearrange("p (u c) -> p c u", u=2)
             nc.scalar.copy(rounded_columns(a, b).bitcast(U32).rearrange("p (c u) -> p c u", u=2), words)
 
-        def quantise(n):
-            first, last = PIECES[n]
-            m = [first >= a and last <= b for a, b in STORES].index(True)
-            a, b = STORES[m]
-            nc.vector.quantize_mx(
-                out=out_codes[m][:, first - a : last - a].bitcast(FP8X4), scales=out_scale[:, first:last], in_=rounded[n][:]
-            )
-            if last == b:
-                nc.sync.dma_start(out=out_words[:, a:b], in_=out_codes[m][:])
-
         def twice(a, b):
             return planes[2][:, a:b].unsqueeze(2).to_broadcast([P, b - a, 2])
 
-        for a, b in EARLY:
+        def round_on_gpsimd(out, in_):
+            nc.gpsimd.tensor_scalar(out, in_, 1.0, -0.0, MULT, ADD)
+
+        for a, b in EARLY + LATE[:-1]:
             for t in range(2):
                 nc.scalar.copy(pairs[a][:, 0, :, t], planes[t][:, a:b])
-        for a, b in LATE:
-            for t in range(2):
-                nc.gpsimd.tensor_scalar(pairs[a][:, 0, :, t], planes[t][:, a:b], 1.0, 0.0, MULT, ADD)
-        for a, b in LATE:
-            nc.gpsimd.tensor_scalar(pairs[a][:, 1], twice(a, b), 1.0, 0.0, MULT, ADD)
+        a, b = LATE[-1]
+        for t in range(2):
+            round_on_gpsimd(pairs[a][:, 0, :, t], planes[t][:, a:b])
+        round_on_gpsimd(pairs[a][:, 1], twice(a, b))
         for a, b in EARLY:
             nc.scalar.copy(pairs[a][:, 1], twice(a, b))
             regroup(a, b)
+        for a, b in LATE[:-1]:
+            nc.scalar.copy(pairs[a][:, 1, :, 0], planes[2][:, a:b])
+
         for a, b in EARLY:
             nc.vector.tensor_copy(
                 rounded_columns(a, b).rearrange("p (c t) -> p c t", t=PACK)[:, :, LAST], planes[LAST][:, a:b]
@@ -238,8 +222,9 @@ def tile_picked_slotadd_tanh_po_kernel(
         for a, b in LATE:
             nc.scalar.copy(pairs[a][:, 1, :, 1], planes[LAST][:, a:b])
             regroup(a, b)
-        for n in range(len(PIECES)):
-            quantise(n)
+        for n, (a, b) in enumerate(PIECES):
+            nc.vector.quantize_mx(out=out_codes[n][:].bitcast(FP8X4), scales=out_scale[:, a:b], in_=rounded[n][:])
+            nc.sync.dma_start(out=out_words[:, a:b], in_=out_codes[n][:])
         for q in range(QUADRANTS):
             queue = nc.scalar if q % 2 == 0 else nc.sync
             queue.dma_start(

from contextlib import ExitStack

import concourse.mybir as mybir

K, T, S, N, U = 512, 2048, 512, 512, 1024
FLOPS = 2 * K * N * S

F32 = mybir.dt.float32
BF16 = mybir.dt.bfloat16
I32 = mybir.dt.int32
U32 = mybir.dt.uint32
U16 = mybir.dt.uint16
U8 = mybir.dt.uint8
FP8X4 = mybir.dt.float8_e4m3fn_x4
ADD = mybir.AluOpType.add
MULT = mybir.AluOpType.mult
COPY = mybir.ActivationFunctionType.Copy
TANH = mybir.ActivationFunctionType.Tanh

P = 128
PACK = 4
LAST = PACK - 1
LIST_ROWS = 16
SCALE_ROWS = K // 32
QUADRANTS = 4
FIRST, SECOND, REST, WHOLE = slice(0, S // 4), slice(S // 4, S // 2), slice(S // 2, S), slice(0, S)
TURN = 3 * S // 8
W_VECTOR = 88
PIECES = ((0, 384), (384, 768), (768, U))
EARLY = ((0, 384), (384, 576))
LATE = ((576, 768), (768, U))
PAIRS_AT = (0, 3072, 4608, 6144)
FROM_AT = (2816, 6144)


def tile_picked_slotadd_tanh_po_kernel(
    tc, x_words, x_scales, w1, mem, offs, slot, from_l, out_0, out_1, out_2
):
    nc = tc.nc
    with ExitStack() as ctx:
        keep = ctx.enter_context(tc.tile_pool(name="keep", bufs=1))
        shared = ctx.enter_context(tc.tile_pool(name="shared", bufs=1))
        psum = ctx.enter_context(tc.psum_pool(name="psum", bufs=1))

        mem_rows = mem.rearrange("(p t) c -> p t c", t=PACK)
        out_rows = out_0.rearrange("(p t) c -> p t c", t=PACK)
        w_rows = w1.rearrange("(p j) c -> p j c", j=PACK)

        def values(name, width, tag=None):
            return keep.tile([P, width], F32, name=name, tag=tag or name, align_bytes=64)

        def entries(places, cols):
            return places[:, cols.start // LIST_ROWS : cols.stop // LIST_ROWS]

        slot_list = keep.tile([P, S // LIST_ROWS], U16, name="slot_list")
        from_list = keep.tile([P, S // LIST_ROWS], U16, name="from_list")
        token_list = keep.tile([P, S // LIST_ROWS], U16, name="token_list")
        planes = [values("plane%d" % t, U) for t in range(2)]
        w_raw = keep.tile([P, PACK, N], F32, name="w_raw", align_bytes=64)

        scale_base = P - SCALE_ROWS
        x_scale_table = keep.tile([P, T], U8, name="x_scale_table", align_bytes=64)
        x_scale_picked = keep.tile([P, S], U8, name="x_scale_picked", align_bytes=64)
        x_scale = keep.tile([P, S], U8, name="x_scale", align_bytes=64)
        nc.scalar.dma_start(out=x_scale_table[scale_base:, :].bitcast(I32), in_=x_scales[0].bitcast(I32))
        warm = keep.tile([P, 2], F32, name="warm")
        nc.vector.memset(warm[:, 0:1], 0.0)
        nc.scalar.activation(warm[:, 1:2], warm[:, 0:1], TANH)
        nc.vector.memset(x_scale_table[:scale_base, :].bitcast(I32), 0)
        nc.vector.memset(x_scale[:].bitcast(I32), 0)

        nc.sync.dma_start(out=planes[0][:], in_=mem_rows[:, 0, :])
        nc.sync.dma_start(slot_list[:], slot)
        nc.sync.dma_start(from_list[:], from_l)
        nc.sync.dma_start(token_list[:], offs)
        nc.sync.dma_start(out=w_raw[:], in_=w_rows)
        nc.sync.dma_start(out=planes[1][:], in_=mem_rows[:, 1, :])
        x_table = keep.tile([P, T], I32, name="x_table", align_bytes=64)
        nc.sync.dma_start(out=x_table[:], in_=x_words[0].rearrange("p c r -> p (c r)").bitcast(I32))

        def look_up(out, t, places, cols=WHOLE):
            nc.scalar.activation(out, planes[t][:].indirect(entries(places, cols)), COPY, scale=0.5)

        def look_up_both(t):
            at_slot, at_from = values("at_slot%d" % t, S), values("at_from%d" % t, S)
            head = slice(0, REST.start)
            nc.vector.tensor_scalar(at_slot[:, head], planes[t][:].indirect(entries(slot_list, head)), 0.5, 0.0, MULT, ADD)
            look_up(at_from[:], t, from_list)
            look_up(at_slot[:, REST], t, slot_list, REST)
            return at_slot, at_from

        at_slot, at_from = look_up_both(0)
        nc.vector.tensor_copy(x_scale_picked[:], x_scale_table[:].indirect(token_list[:]))

        for q in range(QUADRANTS):
            nc.sync.dma_start(
                out=x_scale[32 * q : 32 * q + 4, :].bitcast(I32),
                in_=x_scale_picked[scale_base + 4 * q : scale_base + 4 * q + 4, :].bitcast(I32),
            )

        w_grouped = keep.tile([P, N * PACK], BF16, name="w_grouped", align_bytes=64)
        w_dealt = w_grouped[:].rearrange("p (t m j) -> p m t j", t=PACK, j=PACK)
        w_read = w_raw[:].rearrange("p j (m t) -> p m t j", t=PACK)
        means = [values("mean%d" % t, S) for t in range(2)]
        nc.vector.tensor_tensor(means[0][:], at_slot[:], at_from[:], ADD)
        nc.vector.tensor_copy(w_dealt[:, :W_VECTOR], w_read[:, :W_VECTOR])
        nc.scalar.copy(w_dealt[:, W_VECTOR:], w_read[:, W_VECTOR:])
        for t, tag in enumerate(("x_scale_table", "w_raw"), 2):
            planes.append(values("plane%d" % t, U, tag))
            nc.sync.dma_start(out=planes[t][:], in_=mem_rows[:, t, :])

        x_codes = keep.tile([P, S], U32, name="x_codes", align_bytes=64)
        w_codes = [keep.tile([P, N // 2], U32, name="w_codes%d" % u, align_bytes=64) for u in range(2)]
        w_scale = keep.tile([P, N], U8, name="w_scale", align_bytes=64)
        for u in range(2):
            nc.vector.quantize_mx(
                out=w_codes[u][:].bitcast(FP8X4),
                scales=w_scale[:, u * N // 2 : (u + 1) * N // 2],
                in_=w_grouped[:, u * N * PACK // 2 : (u + 1) * N * PACK // 2],
            )
        at_slot, at_from = look_up_both(1)
        nc.gpsimd.tensor_tensor(means[1][:], at_slot[:], at_from[:], ADD)
        for cols in (FIRST, SECOND, REST):
            nc.vector.tensor_copy(x_codes[:, cols], x_table[:].bitcast(U32).indirect(entries(token_list, cols)))

        def multiply(t, cols, bank=None):
            name = "product%d_%d" % (t, cols.start)
            product = psum.tile([P, cols.stop - cols.start], F32, name=name, tag=bank or name)
            nc.tensor.matmul_mx(
                out=product[:],
                lhsT=w_codes[t // 2][:, t % 2 * P : (t % 2 + 1) * P].bitcast(FP8X4),
                lhsT_scale=w_scale[:, t * P : (t + 1) * P],
                rhs=x_codes[:, cols].bitcast(FP8X4),
                rhs_scale=x_scale[:, cols],
                start=True,
                stop=True,
            )
            return product

        def squash(t, cols, tag=None):
            y = values("y%d_%d" % (t, cols.start), cols.stop - cols.start, tag)
            nc.scalar.activation(y[:], multiply(t, cols)[:], TANH)
            return y

        updates = [values("update%d" % t, S) for t in range(PACK)]

        def add_mean(t, cols, adder):
            adder.tensor_tensor(updates[t][:, cols], squash(t, cols)[:], means[t][:, cols], ADD)

        def scatter(t, cols):
            nc.vector.tensor_copy(planes[t][:].indirect(entries(slot_list, cols)), updates[t][:, cols])
            if cols.stop == S:
                nc.sync.dma_start(out=out_rows[:, t, :], in_=planes[t][:])

        add_mean(0, FIRST, nc.vector)
        add_mean(1, FIRST, nc.vector)
        scatter(0, FIRST)
        add_mean(1, slice(FIRST.stop, TURN), nc.gpsimd)
        scatter(1, slice(0, TURN))
        add_mean(0, SECOND, nc.gpsimd)
        add_mean(0, REST, nc.gpsimd)
        scatter(0, slice(FIRST.stop, S))
        y = values("y1_last", S - TURN)
        nc.scalar.activation(y[:, : REST.start - TURN], multiply(1, slice(TURN, REST.start), "product0_0")[:], TANH)
        nc.scalar.activation(y[:, REST.start - TURN :], multiply(1, REST)[:], TANH)
        nc.gpsimd.tensor_tensor(updates[1][:, TURN:], y[:], means[1][:, TURN:], ADD)
        scatter(1, slice(TURN, S))

        for t, at in enumerate(FROM_AT, 2):
            y = squash(t, WHOLE, "late_y")
            at_slot = values("at_slot%d" % t, S)
            look_up(at_slot[:], t, slot_list)
            partial = values("partial%d" % t, S, "partial")
            nc.gpsimd.tensor_tensor(partial[:], y[:], at_slot[:], ADD)
            at_from = shared.tile([P, S], F32, name="at_from%d" % t, offset=at, align_bytes=64)
            look_up(at_from[:], t, from_list)
            nc.gpsimd.tensor_tensor(updates[t][:], partial[:], at_from[:], ADD)
            scatter(t, WHOLE)

        pairs = {
            a: shared.tile([P, 2, b - a, 2], BF16, name="pairs%d" % a, offset=at, align_bytes=64)
            for (a, b), at in zip(EARLY + LATE, PAIRS_AT)
        }
        rounded = [keep.tile([P, (b - a) * PACK], BF16, name="rounded%d" % a, align_bytes=64) for a, b in PIECES]
        a, b = PIECES[0]
        out_codes = [shared.tile([P, b - a], I32, name="out_codes0", offset=PAIRS_AT[1], align_bytes=64)]
        out_codes.extend(keep.tile([P, b - a], I32, name="out_codes%d" % a, align_bytes=64) for a, b in PIECES[1:])
        out_scale = keep.tile([P, U], U8, name="out_scale", align_bytes=64)
        out_words = out_1[0].rearrange("p c r -> p (c r)").bitcast(I32)

        def rounded_columns(a, b):
            n = [first <= a and b <= last for first, last in PIECES].index(True)
            return rounded[n][:, (a - PIECES[n][0]) * PACK : (b - PIECES[n][0]) * PACK]

        def regroup(a, b):
            words = pairs[a][:].rearrange("p u c e -> p (u c e)").bitcast(U32).rearrange("p (u c) -> p c u", u=2)
            nc.scalar.copy(rounded_columns(a, b).bitcast(U32).rearrange("p (c u) -> p c u", u=2), words)

        def twice(a, b):
            return planes[2][:, a:b].unsqueeze(2).to_broadcast([P, b - a, 2])

        def round_on_gpsimd(out, in_):
            nc.gpsimd.tensor_scalar(out, in_, 1.0, -0.0, MULT, ADD)

        for a, b in EARLY + LATE[:-1]:
            for t in range(2):
                nc.scalar.copy(pairs[a][:, 0, :, t], planes[t][:, a:b])
        a, b = LATE[-1]
        for t in range(2):
            round_on_gpsimd(pairs[a][:, 0, :, t], planes[t][:, a:b])
        round_on_gpsimd(pairs[a][:, 1], twice(a, b))
        for a, b in EARLY:
            nc.scalar.copy(pairs[a][:, 1], twice(a, b))
            regroup(a, b)
        for a, b in LATE[:-1]:
            nc.scalar.copy(pairs[a][:, 1, :, 0], planes[2][:, a:b])

        for a, b in EARLY:
            nc.vector.tensor_copy(
                rounded_columns(a, b).rearrange("p (c t) -> p c t", t=PACK)[:, :, LAST], planes[LAST][:, a:b]
            )
        for a, b in LATE:
            nc.scalar.copy(pairs[a][:, 1, :, 1], planes[LAST][:, a:b])
            regroup(a, b)
        for n, (a, b) in enumerate(PIECES):
            nc.vector.quantize_mx(out=out_codes[n][:].bitcast(FP8X4), scales=out_scale[:, a:b], in_=rounded[n][:])
            nc.sync.dma_start(out=out_words[:, a:b], in_=out_codes[n][:])
        for q in range(QUADRANTS):
            queue = nc.scalar if q % 2 == 0 else nc.sync
            queue.dma_start(
                out=out_2[0, 4 * q : 4 * q + 4, :].bitcast(I32),
                in_=out_scale[32 * q : 32 * q + 4, :].bitcast(I32),
            )
